import numpy as np
import ml_dtypes


def mxq(x, axis, fmt="e4m3"):
    dtype, down = {"e4m3": (ml_dtypes.float8_e4m3fn, 7), "e5m2": (ml_dtypes.float8_e5m2, 14)}[fmt]
    v = np.moveaxis(np.asarray(x, np.float32).astype(ml_dtypes.bfloat16).astype(np.float64), axis, -1)
    blocks = v.reshape(v.shape[:-1] + (-1, 32))
    amax = np.abs(blocks).max(-1, keepdims=True)
    byte = np.maximum(np.where(amax > 0, np.frexp(amax)[1] - 1 + 127, 0) - down, 1)
    scale = np.exp2(byte - 127.0)
    codes = (blocks / scale).astype(np.float32).astype(dtype).astype(np.float64)
    return np.moveaxis((codes * scale).reshape(v.shape), -1, axis)


WIDE = False


def mx_kscale(k):
    if not WIDE:
        return np.ones(k)
    levels = np.array([10, -10, 5, -5, 0])
    if k % 512:
        return np.exp2(np.random.permutation(np.resize(levels, k // 32))).repeat(32)
    a = np.empty((k // 512, 16))
    for p in range(k // 512):
        a[p, :8] = np.random.permutation(np.resize(levels, 8))
        for g in range(8):
            far = levels[np.abs(levels - a[p, g]) >= 10]
            a[p, g + 8] = far[np.random.randint(len(far))]
    return np.exp2(a.ravel()).repeat(32)


BF16 = ml_dtypes.bfloat16


def bf(x):
    return np.asarray(x, np.float32).astype(BF16)


def f64(x):
    return np.asarray(x).astype(np.float64)


N, D, F, E = 1024, 512, 512, 4


def draw0():
    s, t = mx_kscale(D), mx_kscale(N)
    x = np.random.standard_normal((N, D)) * s
    a = np.random.standard_normal((E, N, N)) * (1.5 / np.sqrt(N)) / t
    w = np.random.standard_normal((E, D, F)) * (1.5 / np.sqrt(D)) / s[:, None]
    c = (1.0 + 0.1 * np.random.standard_normal(N)) * t
    b = np.random.standard_normal((E, F)) * 0.5
    wg = np.random.standard_normal((D, E)) * (2.0 / np.sqrt(D)) / s[:, None]
    w0 = np.random.standard_normal((D, F)) * (0.7 / np.sqrt(D)) / s[:, None]
    return {"x": bf(x), "a": bf(a), "w": bf(w), "c": bf(c), "b": bf(b), "wg": bf(wg), "w0": bf(w0)}


def gate_weights(x, wg):
    z = np.sum(x[:, None, :] * wg.T[None, :, :], axis=-1)
    u = np.exp(z - z.max(axis=-1, keepdims=True))
    return u / u.sum(axis=-1, keepdims=True)


def relation_experts(xq, a, w, c, b):
    p = c[None, :, None] * (xq @ mxq(w, 1, "e4m3"))
    agg = mxq(a, 2, "e4m3") @ mxq(p, 1, "e4m3")
    return np.maximum(agg + b[:, None, :], 0.0)


def core(x, a, w, c, b, wg, w0):
    x = f64(x)
    g = gate_weights(x, f64(wg))
    xq = mxq(x, 1, "e4m3")
    h = relation_experts(xq, f64(a), f64(w), f64(c), f64(b))
    r = xq @ mxq(f64(w0), 0, "e4m3")
    return r + np.sum(g.T[:, :, None] * h, axis=0)


def e4m3fn_bytes(y):
    return np.clip(np.asarray(y, np.float64), -448.0, 448.0).astype(np.float32).astype(ml_dtypes.float8_e4m3fn).view(np.uint8)


def e4m3fn_values(b):
    return np.asarray(b, np.uint8).view(ml_dtypes.float8_e4m3fn).astype(np.float64)


def setup_inputs():
    d = draw0()
    x0 = np.asarray(d['a']).astype(np.float64)
    s = (np.max(np.abs(x0), axis=(0, 1), keepdims=True) / 448.0).astype(np.float32)
    out = {}
    for k, v in d.items():
        if k == 'a':
            out['a_bytes'] = e4m3fn_bytes(x0 / s.astype(np.float64))
            out['a_scale'] = s
        else:
            out[k] = v
    return out


def reference(x, a_bytes, a_scale, w, c, b, wg, w0):
    return core(x, e4m3fn_values(a_bytes) * a_scale.astype(np.float64), w, c, b, wg, w0)

@@ -1,0 +1,367 @@
+from contextlib import ExitStack
+
+import concourse.mybir as mybir
+from concourse.masks import make_identity
+
+N, D, F, E = 1024, 512, 512, 4
+FLOPS = 2 * N * D * F * (E + 1) + 2 * E * N * N * F + 2 * N * D * E
+
+F32 = mybir.dt.float32
+BF16 = mybir.dt.bfloat16
+U32 = mybir.dt.uint32
+U8 = mybir.dt.uint8
+FP8 = mybir.dt.float8_e4m3fn
+FP8X4 = mybir.dt.float8_e4m3fn_x4
+ALU = mybir.AluOpType
+ACT = mybir.ActivationFunctionType
+AX = mybir.AxisListType
+
+P = 128
+PACK = 4
+HALF = P * PACK
+HALVES = N // HALF
+UNITS = E * HALVES
+WIDEN_LAST = 33
+PROJ_FIRST = 4
+PROJ_BURST = 3
+PROJ_HEAD = 16
+PROJ_LAG = -3
+S_PARTS = 2
+HEAD_LOADS = "a0 x0 w0 x1"
+REST_LOADS = "w4 a1 w1 a2 a3 w2 w3"
+RES_INIT = True
+SHARED = 0
+W0_AT = 0
+AGG_FIRST = 9
+AGG_LAST = 39
+MIX_LAG = 6
+RES_FIRST = 6
+W_QUANT_LEAD = 2
+W_GROUP_LEAD = 2
+P_ILV = "VVVVVVSS"
+W_ILV = "VVVSS"
+BANKS = {"turn":2,"mx":3,"back":3}
+GATE_LAG = 2
+P_GROUP_LAG = 1
+P_QUANT_LAG = 1
+A_QUANT_LAG = 2
+GROUP_BUFS = 2
+S_PSUM = False
+
+
+def tile_relationalgraphmixtureofexperts_kernel(tc, x, a_bytes, a_scale, w, c, b, wg, w0, out):
+    nc = tc.nc
+    with ExitStack() as ctx:
+        keep = ctx.enter_context(tc.tile_pool(name="keep", bufs=1))
+        flow = ctx.enter_context(tc.tile_pool(name="flow", bufs=2))
+        psum = ctx.enter_context(tc.psum_pool(name="psum", bufs=2))
+        ctx.enter_context(tc.manual_schedule())
+
+        def bank(tag):
+            if SHARED:
+                return psum.tile([P, HALF], F32, name="any", tag="any", bufs=SHARED)
+            return psum.tile([P, HALF], F32, name=tag, tag=tag, bufs=BANKS[tag])
+
+        def quantise(grouped, tag, bufs):
+            width = grouped.shape[1] // PACK
+            codes = flow.tile([P, width], U32, name=tag + "_codes", tag=tag + "_codes", bufs=bufs, align_bytes=64)
+            scales = flow.tile([P, width], U8, name=tag + "_scales", tag=tag + "_scales", bufs=bufs, align_bytes=64)
+            nc.vector.quantize_mx(out=codes[:].bitcast(FP8X4), scales=scales[:], in_=grouped)
+            return codes, scales
+
+        def mx(dst, still, still_cols, moving, moving_cols, start, stop):
+            nc.tensor.matmul_mx(
+                out=dst,
+                lhsT=still[0][:, still_cols].bitcast(FP8X4),
+                lhsT_scale=still[1][:, still_cols],
+                rhs=moving[0][:, moving_cols].bitcast(FP8X4),
+                rhs_scale=moving[1][:, moving_cols],
+                start=start,
+                stop=stop,
+            )
+
+        def cols(i, width):
+            return slice(i * width, (i + 1) * width)
+
+        def interleave(engine, grouped, planes, part):
+            dst = grouped[:].rearrange("p (c i t) -> p c t i", i=4, t=PACK)[:, part]
+            src = planes[:].rearrange("p t (c i) -> p c t i", i=4)[:, part]
+            if engine == "S":
+                nc.scalar.copy(out=dst, in_=src)
+            elif engine == "V":
+                nc.vector.tensor_copy(out=dst, in_=src)
+            else:
+                dst = grouped[:].rearrange("p (n t) -> p n t", t=PACK)
+                src = planes[:].rearrange("p t n -> p n t")
+                nc.gpsimd.tensor_scalar(out=dst, in0=src, scalar1=1.0, scalar2=0.0, op0=ALU.mult, op1=ALU.add)
+
+        a_raw, w_raw, x_raw = {}, {}, {}
+
+        def load_a(unit):
+            e, h = divmod(unit, HALVES)
+            a_raw[unit] = flow.tile([P, PACK * N], U8, name="a_raw", tag="a_raw", bufs=4, align_bytes=64)
+            nc.sync.dma_start(out=a_raw[unit][:], in_=a_bytes[e, cols(h, HALF), :].rearrange("(p t) m -> p (t m)", t=PACK))
+
+        def load_w(e):
+            src = w0 if e == E else w[e]
+            w_raw[e] = keep.tile([P, PACK, F], BF16, name="w_raw%d" % e, align_bytes=64)
+            nc.sync.dma_start(out=w_raw[e][:], in_=src.rearrange("(p t) f -> p t f", t=PACK))
+
+        def load_x(h):
+            x_raw[h] = keep.tile([P, PACK, D], BF16, name="x_raw%d" % h, align_bytes=64)
+            nc.sync.dma_start(out=x_raw[h][:], in_=x[cols(h, HALF), :].rearrange("(p t) d -> p t d", t=PACK))
+
+        ident = keep.tile([P, P], F32, name="ident", align_bytes=64)
+        make_identity(nc, ident[:])
+        b_wide = keep.tile([P, P], F32, name="b_wide", align_bytes=64)
+        nc.gpsimd.memset(b_wide[:], 0.0)
+
+        s_rows = keep.tile([P, P], F32, name="s_rows", align_bytes=64)
+        nc.vector.memset(s_rows[:], 0.0)
+        s_src = a_scale.rearrange("i j (r q u e) -> u (i j r) q e", r=4, u=2, e=2)
+        for u in range(2):
+            nc.sync.dma_start(out=s_rows[cols(u, 4), :].rearrange("r (q e) -> r q e", e=2), in_=s_src[u])
+        for item in HEAD_LOADS.split():
+            {"a": load_a, "x": load_x, "w": load_w}[item[0]](int(item[1]))
+        wg_sb = keep.tile([P, PACK, E], BF16, name="wg_sb", align_bytes=64)
+        nc.sync.dma_start(out=wg_sb[:], in_=wg.rearrange("(p t) e -> p t e", t=PACK))
+        c_raw = keep.tile([P, HALVES, PACK], BF16, name="c_raw", align_bytes=64)
+        nc.sync.dma_start(out=c_raw[:], in_=c.rearrange("(g p t) -> p g t", p=P, t=PACK))
+        b_rows = keep.tile([E * PACK, P], BF16, name="b_rows", align_bytes=64)
+        nc.sync.dma_start(out=b_rows[:], in_=b.rearrange("e (j p) -> (e j) p", p=P))
+        for item in REST_LOADS.split():
+            {"a": load_a, "x": load_x, "w": load_w}[item[0]](int(item[1]))
+
+        back = bank("back")
+        nc.tensor.transpose(back[:, cols(0, P)], s_rows[:], ident[:])
+        s_cols = keep.tile([P, 8], F32, name="s_cols", align_bytes=64)
+        nc.scalar.copy(out=s_cols[:], in_=back[:, :8])
+        s_half = []
+        s_perm = keep.tile([P, N], F32, name="s_perm", align_bytes=64)
+        for u in range(2):
+            spread = psum.tile([P, HALF], F32, name="s_spread%d" % u, bufs=1) if S_PSUM else bank("mx")
+            for r in range(4):
+                nc.tensor.transpose(spread[:, cols(r, P)], s_cols[:, 4 * u + r : 4 * u + r + 1].to_broadcast([P, P]), ident[:])
+            s_half.append(spread[:])
+            if not S_PSUM:
+                nc.scalar.copy(out=s_perm[:, cols(u, HALF)], in_=spread[:])
+
+        a_wide, a_turned, a_mx = {}, {}, {}
+        x_turned, x_mx, w_grouped, w_mx = {}, {}, {}, {}
+        p_planes, p_grouped, p_mx, h_rows, acc = {}, {}, {}, {}, {}
+        held = {}
+
+        def widen_a(i):
+            unit, t = divmod(i, PACK)
+            a_wide[i] = flow.tile([P, N], BF16, name="a_wide", tag="a_wide", bufs=4, align_bytes=64)
+            codes = a_raw[unit][:, cols(t, N)].bitcast(FP8).rearrange("p (q u e) -> p u q e", u=2, e=2)
+            wide = a_wide[i][:].rearrange("p (u q e) -> p u q e", u=2, e=2)
+            if S_PSUM:
+                for u in range(2):
+                    nc.vector.tensor_tensor(out=wide[:, u], in0=codes[:, u], in1=s_half[u].rearrange("p (q e) -> p q e", e=2), op=ALU.mult)
+            else:
+                nc.vector.tensor_tensor(out=wide, in0=codes, in1=s_perm[:].rearrange("p (u q e) -> p u q e", u=2, e=2), op=ALU.mult)
+            if t == PACK - 1 and unit + 4 < UNITS:
+                load_a(unit + 4)
+
+        def turn_a(i):
+            words = a_wide[i][:].bitcast(F32)
+            turned = bank("turn")
+            for g in range(HALVES):
+                for u in range(2):
+                    nc.tensor.transpose(turned[:, cols(2 * g + u, P)], words[:, cols(2 * u + g, P)], ident[:])
+            held["a", i] = turned
+
+        def copy_a(i):
+            unit, t = divmod(i, PACK)
+            if t == 0:
+                a_turned[unit] = flow.tile([P, PACK * N], BF16, name="a_turned", tag="a_turned", bufs=2, align_bytes=64)
+            dst = a_turned[unit][:].bitcast(F32).rearrange("p (g t r u) -> p g t r u", g=HALVES, t=PACK, u=2)
+            nc.scalar.copy(out=dst[:, :, t], in_=held["a", i][:].rearrange("p (g u r) -> p g r u", g=HALVES, u=2))
+
+        def turn_x(h, pair):
+            words = x_raw[h][:].bitcast(F32)
+            turned = bank("turn")
+            for s in range(2):
+                for u in range(2):
+                    nc.tensor.transpose(turned[:, cols(2 * s + u, P)], words[:, 2 * pair + s, u::2], ident[:])
+            if pair == 0:
+                x_turned[h] = keep.tile([P, PACK * HALF], BF16, name="x_turned%d" % h, align_bytes=64)
+            dst = x_turned[h][:].bitcast(F32).rearrange("p (t r u) -> p t r u", t=PACK, u=2)
+            nc.scalar.copy(out=dst[:, 2 * pair : 2 * pair + 2], in_=turned[:].rearrange("p (s u r) -> p s r u", s=2, u=2))
+
+        def parts(engine):
+            return S_PARTS if engine == "S" else 1
+
+        def group_w(e, part):
+            if part == 0:
+                w_grouped[e] = flow.tile([P, PACK * F], BF16, name="w_grouped", tag="w_grouped", bufs=GROUP_BUFS, align_bytes=64)
+            if part < parts(W_ILV[e]):
+                interleave(W_ILV[e], w_grouped[e], w_raw[e], cols(part, F // 4 // parts(W_ILV[e])))
+
+        def project(i):
+            v, t = divmod(i, PACK)
+            e, g = divmod(v, HALVES)
+            proj = bank("mx")
+            mx(proj[:], x_mx[g], cols(t, P), w_mx[e], cols(0, F), True, True)
+            if t == 0:
+                p_planes[v] = flow.tile([P, PACK, F], BF16, name="p_planes", tag="p_planes", bufs=3, align_bytes=64)
+            nc.scalar.activation(out=p_planes[v][:, t, :], in_=proj[:], func=ACT.Copy, scale=c32[:, PACK * g + t : PACK * g + t + 1])
+
+        def group_p(v, part):
+            if part == 0:
+                p_grouped[v] = flow.tile([P, PACK * F], BF16, name="p_grouped", tag="p_grouped", bufs=GROUP_BUFS, align_bytes=64)
+            if part < parts(P_ILV[v]):
+                interleave(P_ILV[v], p_grouped[v], p_planes[v], cols(part, F // 4 // parts(P_ILV[v])))
+
+        def aggregate(i):
+            unit, j = divmod(i, PACK)
+            e = unit // HALVES
+            agg = bank("mx")
+            for g in range(HALVES):
+                mx(agg[:], p_mx[HALVES * e + g], cols(j, P), a_mx[unit], cols(g, HALF), g == 0, g == HALVES - 1)
+            if j == 0:
+                h_rows[unit] = flow.tile([P, PACK, HALF], F32, name="h_rows", tag="h_rows", bufs=3, align_bytes=64)
+            nc.scalar.activation(out=h_rows[unit][:, j, :], in_=agg[:], func=ACT.Relu, bias=b_cols[:, PACK * e + j : PACK * e + j + 1])
+
+        def turn_h(i):
+            unit, t = divmod(i, PACK)
+            back = bank("back")
+            for j in range(PACK):
+                nc.tensor.transpose(back[:, cols(j, P)], h_rows[unit][:, j, cols(t, P)], ident[:])
+            held["h", i] = back
+
+        def store(tile):
+            h, t = divmod(tile, PACK)
+            nc.sync.dma_start(out=out[cols(h, HALF), :].rearrange("(p t) f -> p t f", t=PACK)[:, t, :], in_=acc[tile][:])
+
+        def mix(i):
+            unit, t = divmod(i, PACK)
+            e, h = divmod(unit, HALVES)
+            tile = PACK * h + t
+            weight = gate[:, tile, e : e + 1]
+            if e == 0 and not RES_INIT:
+                acc[tile] = keep.tile([P, F], F32, name="acc%d" % tile, align_bytes=64)
+                nc.scalar.activation(out=acc[tile][:], in_=held["h", i][:], func=ACT.Copy, scale=weight)
+            else:
+                nc.vector.scalar_tensor_tensor(
+                    out=acc[tile][:], in0=held["h", i][:], scalar=weight, in1=acc[tile][:], op0=ALU.mult, op1=ALU.add
+                )
+            if e == E - 1:
+                store(tile)
+
+        def residual(tile):
+            h, t = divmod(tile, PACK)
+            res = bank("mx")
+            mx(res[:], x_mx[h], cols(t, P), w_mx[E], cols(0, F), True, True)
+            if RES_INIT:
+                acc[tile] = keep.tile([P, F], F32, name="acc%d" % tile, align_bytes=64)
+                nc.scalar.copy(out=acc[tile][:], in_=res[:])
+            else:
+                nc.vector.tensor_tensor(out=acc[tile][:], in0=res[:], in1=acc[tile][:], op=ALU.add)
+
+        c32 = keep.tile([P, HALVES * PACK], F32, name="c32", align_bytes=64)
+        b_cols = keep.tile([P, E * PACK], F32, name="b_cols", align_bytes=64)
+        gate = keep.tile([P, HALVES * PACK, E], F32, name="gate", align_bytes=64)
+
+        def constants():
+            nc.scalar.copy(out=c32[:], in_=c_raw[:].rearrange("p g t -> p (g t)"))
+            nc.scalar.copy(out=b_wide[: E * PACK, :], in_=b_rows[:])
+            back = bank("back")
+            nc.tensor.transpose(back[:, cols(0, P)], b_wide[:], ident[:])
+            nc.scalar.copy(out=b_cols[:], in_=back[:, : E * PACK])
+
+        def gate_logits(tile):
+            if tile == 0:
+                logits = bank("back")
+                held["logits"] = logits[:, : HALVES * PACK * E].rearrange("p (n e) -> p n e", e=E)
+            h, t = divmod(tile, PACK)
+            planes = x_turned[h][:].rearrange("p (n s) -> p n s", s=PACK)
+            for s in range(PACK):
+                nc.tensor.matmul(
+                    held["logits"][:, tile, :], lhsT=planes[:, cols(t, P), s], rhs=wg_sb[:, s, :], start=s == 0, stop=s == PACK - 1
+                )
+
+        shape = [P, HALVES * PACK, E]
+        top = keep.tile(shape[:2], F32, name="top", align_bytes=64)
+        shifted = keep.tile(shape, F32, name="shifted", align_bytes=64)
+        expo = keep.tile(shape, F32, name="expo", align_bytes=64)
+        total = keep.tile(shape[:2], F32, name="total", align_bytes=64)
+        inverse = keep.tile(shape[:2], F32, name="inverse", align_bytes=64)
+
+        def softmax_step(step):
+            if step == 0:
+                nc.vector.tensor_reduce(out=top[:], in_=held["logits"], axis=AX.X, op=ALU.max)
+            elif step == 1:
+                nc.vector.tensor_tensor(out=shifted[:], in0=held["logits"], in1=top[:].unsqueeze(2).to_broadcast(shape), op=ALU.subtract)
+                nc.scalar.activation(out=expo[:], in_=shifted[:], func=ACT.Exp)
+            elif step == 2:
+                nc.vector.tensor_reduce(out=total[:], in_=expo[:], axis=AX.X, op=ALU.add)
+            elif step == 3:
+                nc.vector.reciprocal(out=inverse[:], in_=total[:])
+            else:
+                nc.vector.tensor_tensor(out=gate[:], in0=expo[:], in1=inverse[:].unsqueeze(2).to_broadcast(shape), op=ALU.mult)
+
+        steps = UNITS * PACK
+
+        def due(slot, slots):
+            return [i for i, s in enumerate(slots) if s == slot]
+
+        def paced(first, last):
+            return [first + i * (last - first) // (steps - 1) for i in range(steps)]
+
+        def after(slots, lag):
+            return [s + lag for s in slots[PACK - 1 :: PACK]]
+
+        widen_at = paced(0, WIDEN_LAST)
+        project_at = [PROJ_FIRST + i // PROJ_BURST if i < PROJ_HEAD else PROJ_LAG + i for i in range(steps)]
+        aggregate_at = paced(AGG_FIRST, AGG_LAST)
+        mix_at = paced(AGG_FIRST + MIX_LAG, AGG_LAST + MIX_LAG)
+        w_quant_at = [s - W_QUANT_LEAD for s in project_at[2 * PACK :: 2 * PACK]] + [RES_FIRST - W_QUANT_LEAD]
+
+        p_quant_at = [s + P_GROUP_LAG + P_QUANT_LAG + parts(P_ILV[v]) - 1 for v, s in enumerate(after(project_at, 0))]
+        assert W_GROUP_LEAD >= S_PARTS
+        assert all(RES_FIRST + i < s for i, s in enumerate(mix_at[-HALVES * PACK :]))
+        for slot in range(mix_at[-1] + 1):
+            for i in due(slot, widen_at):
+                widen_a(i)
+            for h in due(slot, range(HALVES)):
+                turn_x(h, 0)
+                turn_x(h, 1)
+            if slot == W0_AT:
+                for part in range(S_PARTS):
+                    group_w(0, part)
+            for i in due(slot + 1, mix_at):
+                turn_h(i)
+            for i in due(slot - 1, widen_at):
+                turn_a(i)
+                copy_a(i)
+            for h in due(slot - 1, range(HALVES)):
+                x_mx[h] = quantise(x_turned[h][:], "x", 2)
+            if slot == W0_AT + 1:
+                w_mx[0] = quantise(w_grouped[0][:], "w", 3)
+            if slot == 1:
+                constants()
+            for i in due(slot, mix_at):
+                mix(i)
+            for i in due(slot, aggregate_at):
+                aggregate(i)
+            for i in due(slot, project_at):
+                project(i)
+            for tile in due(slot - RES_FIRST, range(HALVES * PACK)):
+                residual(tile)
+            for tile in due(slot - GATE_LAG, range(HALVES * PACK)):
+                gate_logits(tile)
+            for step in due(slot - GATE_LAG - HALVES * PACK, range(5)):
+                softmax_step(step)
+            for unit in due(slot, after(widen_at, A_QUANT_LAG)):
+                a_mx[unit] = quantise(a_turned[unit][:], "a", 4)
+            for e in due(slot, w_quant_at):
+                w_mx[e + 1] = quantise(w_grouped[e + 1][:], "w", 3)
+            for v in due(slot, p_quant_at):
+                p_mx[v] = quantise(p_grouped[v][:], "p", UNITS)
+            for part in range(S_PARTS):
+                for v in due(slot - part, after(project_at, P_GROUP_LAG)):
+                    group_p(v, part)
+                for e in due(slot - part + W_GROUP_LEAD, w_quant_at):
+                    group_w(e + 1, part)

@@ -21,32 +21,36 @@ PACK = 4
 HALF = P * PACK
 HALVES = N // HALF
 UNITS = E * HALVES
-WIDEN_LAST = 33
-PROJ_FIRST = 4
-PROJ_BURST = 3
-PROJ_HEAD = 16
-PROJ_LAG = -3
-S_PARTS = 2
-HEAD_LOADS = "a0 x0 w0 x1"
-REST_LOADS = "w4 a1 w1 a2 a3 w2 w3"
+AGG_LAG = 7
+A_Q = 6
+FIRST = 6
+MIX_LAG = 8
+PROJ_SECOND = 7
+PROJ_SPAN = 4
+PROJ_LEAD = 5
+P1_ENG = "GG"
+RES_FIRST = 11
+RES_UNIT = 1
 RES_INIT = True
-SHARED = 0
-W0_AT = 0
-AGG_FIRST = 9
-AGG_LAST = 39
-MIX_LAG = 6
-RES_FIRST = 6
-W_QUANT_LEAD = 2
-W_GROUP_LEAD = 2
-P_ILV = "VVVVVVSS"
-W_ILV = "VVVSS"
-BANKS = {"turn":2,"mx":3,"back":3}
-GATE_LAG = 2
-P_GROUP_LAG = 1
-P_QUANT_LAG = 1
-A_QUANT_LAG = 2
-GROUP_BUFS = 2
-S_PSUM = False
+RES_ON_VECTOR = ()
+RES_SKIP = 1
+FIRST_ON_SCALAR = ()
+GATE_AT = (-1, -1, 6, 6, 9, 10, 11, 12)
+SM_END = (1, 2)
+WIDE_BUFS = 6
+H_BUFS = 4
+GROUP_BUFS = 1
+PROLOGUE = 'I0 x0 x1 a0 a1 x2 x3 c0 X0 a2 X1 W0 G1 t0 t1 p0 p1 p2 p3 p4 p5 p6 p7 a3 a4 t2 t3 a5 W1 J0 g0 g1 p8 p9 p10 p11 J1 A0 t4 P0 G2 G4'
+BANKS = {"turn": 2, "mx": 2, "back": 2}
+HEAD_LOADS = 'w0 x0 x1 a0'
+REST_LOADS = 'w1 a1 w2 w4 a2 a3 w3'
+SHARED = 4
+RING_W = True
+AGG_CATCH = (21,)
+EARLY_A = 6
+LAST_P = 29
+MIX_CATCH = (18, 22)
+S_PSUM = True
 
 
 def tile_relationalgraphmixtureofexperts_kernel(tc, x, a_bytes, a_scale, w, c, b, wg, w0, out):
@@ -58,7 +62,7 @@ def tile_relationalgraphmixtureofexperts_kernel(tc, x, a_bytes, a_scale, w, c, b
         ctx.enter_context(tc.manual_schedule())
 
         def bank(tag):
-            if SHARED:
+            if SHARED and tag != "back":
                 return psum.tile([P, HALF], F32, name="any", tag="any", bufs=SHARED)
             return psum.tile([P, HALF], F32, name=tag, tag=tag, bufs=BANKS[tag])
 
@@ -83,17 +87,18 @@ def tile_relationalgraphmixtureofexperts_kernel(tc, x, a_bytes, a_scale, w, c, b
         def cols(i, width):
             return slice(i * width, (i + 1) * width)
 
-        def interleave(engine, grouped, planes, part):
-            dst = grouped[:].rearrange("p (c i t) -> p c t i", i=4, t=PACK)[:, part]
-            src = planes[:].rearrange("p t (c i) -> p c t i", i=4)[:, part]
-            if engine == "S":
-                nc.scalar.copy(out=dst, in_=src)
-            elif engine == "V":
-                nc.vector.tensor_copy(out=dst, in_=src)
-            else:
-                dst = grouped[:].rearrange("p (n t) -> p n t", t=PACK)
-                src = planes[:].rearrange("p t n -> p n t")
+        def interleave(engine, grouped, planes):
+            if engine == "G":
+                dst = grouped.rearrange("p (n t) -> p n t", t=PACK)
+                src = planes.rearrange("p t n -> p n t")
                 nc.gpsimd.tensor_scalar(out=dst, in0=src, scalar1=1.0, scalar2=0.0, op0=ALU.mult, op1=ALU.add)
+            else:
+                dst = grouped.rearrange("p (c i t) -> p c t i", i=4, t=PACK)
+                src = planes.rearrange("p t (c i) -> p c t i", i=4)
+                if engine == "S":
+                    nc.scalar.copy(out=dst, in_=src)
+                else:
+                    nc.vector.tensor_copy(out=dst, in_=src)
 
         a_raw, w_raw, x_raw = {}, {}, {}
 
@@ -116,11 +121,8 @@ def tile_relationalgraphmixtureofexperts_kernel(tc, x, a_bytes, a_scale, w, c, b
         b_wide = keep.tile([P, P], F32, name="b_wide", align_bytes=64)
         nc.gpsimd.memset(b_wide[:], 0.0)
 
-        s_rows = keep.tile([P, P], F32, name="s_rows", align_bytes=64)
-        nc.vector.memset(s_rows[:], 0.0)
-        s_src = a_scale.rearrange("i j (r q u e) -> u (i j r) q e", r=4, u=2, e=2)
-        for u in range(2):
-            nc.sync.dma_start(out=s_rows[cols(u, 4), :].rearrange("r (q e) -> r q e", e=2), in_=s_src[u])
+        s_cols = keep.tile([P, HALVES, PACK], F32, name="s_cols", align_bytes=64)
+        nc.sync.dma_start(out=s_cols[:], in_=a_scale.rearrange("i j (g p t) -> p (i j g) t", p=P, t=PACK))
         for item in HEAD_LOADS.split():
             {"a": load_a, "x": load_x, "w": load_w}[item[0]](int(item[1]))
         wg_sb = keep.tile([P, PACK, E], BF16, name="wg_sb", align_bytes=64)
@@ -132,19 +134,12 @@ def tile_relationalgraphmixtureofexperts_kernel(tc, x, a_bytes, a_scale, w, c, b
         for item in REST_LOADS.split():
             {"a": load_a, "x": load_x, "w": load_w}[item[0]](int(item[1]))
 
-        back = bank("back")
-        nc.tensor.transpose(back[:, cols(0, P)], s_rows[:], ident[:])
-        s_cols = keep.tile([P, 8], F32, name="s_cols", align_bytes=64)
-        nc.scalar.copy(out=s_cols[:], in_=back[:, :8])
         s_half = []
-        s_perm = keep.tile([P, N], F32, name="s_perm", align_bytes=64)
-        for u in range(2):
-            spread = psum.tile([P, HALF], F32, name="s_spread%d" % u, bufs=1) if S_PSUM else bank("mx")
-            for r in range(4):
-                nc.tensor.transpose(spread[:, cols(r, P)], s_cols[:, 4 * u + r : 4 * u + r + 1].to_broadcast([P, P]), ident[:])
+        for g in range(HALVES):
+            spread = psum.tile([P, HALF], F32, name="s_spread%d" % g, bufs=1)
+            for t in range(PACK):
+                nc.tensor.transpose(spread[:, t::PACK], s_cols[:, g, t : t + 1].to_broadcast([P, P]), ident[:])
             s_half.append(spread[:])
-            if not S_PSUM:
-                nc.scalar.copy(out=s_perm[:, cols(u, HALF)], in_=spread[:])
 
         a_wide, a_turned, a_mx = {}, {}, {}
         x_turned, x_mx, w_grouped, w_mx = {}, {}, {}, {}
@@ -153,14 +148,10 @@ def tile_relationalgraphmixtureofexperts_kernel(tc, x, a_bytes, a_scale, w, c, b
 
         def widen_a(i):
             unit, t = divmod(i, PACK)
-            a_wide[i] = flow.tile([P, N], BF16, name="a_wide", tag="a_wide", bufs=4, align_bytes=64)
-            codes = a_raw[unit][:, cols(t, N)].bitcast(FP8).rearrange("p (q u e) -> p u q e", u=2, e=2)
-            wide = a_wide[i][:].rearrange("p (u q e) -> p u q e", u=2, e=2)
-            if S_PSUM:
-                for u in range(2):
-                    nc.vector.tensor_tensor(out=wide[:, u], in0=codes[:, u], in1=s_half[u].rearrange("p (q e) -> p q e", e=2), op=ALU.mult)
-            else:
-                nc.vector.tensor_tensor(out=wide, in0=codes, in1=s_perm[:].rearrange("p (u q e) -> p u q e", u=2, e=2), op=ALU.mult)
+            a_wide[i] = flow.tile([P, N], BF16, name="a_wide", tag="a_wide", bufs=WIDE_BUFS, align_bytes=64)
+            codes = a_raw[unit][:, cols(t, N)].bitcast(FP8)
+            for g in range(HALVES):
+                nc.vector.tensor_tensor(out=a_wide[i][:, cols(g, HALF)], in0=codes[:, cols(g, HALF)], in1=s_half[g], op=ALU.mult)
             if t == PACK - 1 and unit + 4 < UNITS:
                 load_a(unit + 4)
 
@@ -169,7 +160,7 @@ def tile_relationalgraphmixtureofexperts_kernel(tc, x, a_bytes, a_scale, w, c, b
             turned = bank("turn")
             for g in range(HALVES):
                 for u in range(2):
-                    nc.tensor.transpose(turned[:, cols(2 * g + u, P)], words[:, cols(2 * u + g, P)], ident[:])
+                    nc.tensor.transpose(turned[:, cols(2 * g + u, P)], words[:, 2 * P * g + u : 2 * P * (g + 1) : 2], ident[:])
             held["a", i] = turned
 
         def copy_a(i):
@@ -190,38 +181,40 @@ def tile_relationalgraphmixtureofexperts_kernel(tc, x, a_bytes, a_scale, w, c, b
             dst = x_turned[h][:].bitcast(F32).rearrange("p (t r u) -> p t r u", t=PACK, u=2)
             nc.scalar.copy(out=dst[:, 2 * pair : 2 * pair + 2], in_=turned[:].rearrange("p (s u r) -> p s r u", s=2, u=2))
 
-        def parts(engine):
-            return S_PARTS if engine == "S" else 1
+        def group_w(e, engine):
+            if e == E:
+                w_grouped[e] = keep.tile([P, PACK * F], BF16, name="w4_grouped", align_bytes=64)
+            elif e < 2 and not RING_W:
+                w_grouped[e] = keep.tile([P, PACK * F], BF16, name="w%d_grouped" % e, align_bytes=64)
+            else:
+                w_grouped[e] = flow.tile([P, HALVES * PACK * F], BF16, name="grouped", tag="grouped", bufs=GROUP_BUFS, align_bytes=64)
+            interleave(engine, w_grouped[e][:, : PACK * F], w_raw[e][:])
 
-        def group_w(e, part):
-            if part == 0:
-                w_grouped[e] = flow.tile([P, PACK * F], BF16, name="w_grouped", tag="w_grouped", bufs=GROUP_BUFS, align_bytes=64)
-            if part < parts(W_ILV[e]):
-                interleave(W_ILV[e], w_grouped[e], w_raw[e], cols(part, F // 4 // parts(W_ILV[e])))
+        def quantise_w(e):
+            w_mx[e] = quantise(w_grouped[e][:, : PACK * F], "w", 3)
 
         def project(i):
-            v, t = divmod(i, PACK)
-            e, g = divmod(v, HALVES)
+            e, left = divmod(i, HALVES * PACK)
+            g, t = divmod(left, PACK)
             proj = bank("mx")
             mx(proj[:], x_mx[g], cols(t, P), w_mx[e], cols(0, F), True, True)
             if t == 0:
-                p_planes[v] = flow.tile([P, PACK, F], BF16, name="p_planes", tag="p_planes", bufs=3, align_bytes=64)
-            nc.scalar.activation(out=p_planes[v][:, t, :], in_=proj[:], func=ACT.Copy, scale=c32[:, PACK * g + t : PACK * g + t + 1])
+                p_planes[e, g] = flow.tile([P, PACK, F], BF16, name="p_planes", tag="p_planes", bufs=3, align_bytes=64)
+            nc.scalar.activation(out=p_planes[e, g][:, t, :], in_=proj[:], func=ACT.Copy, scale=c32[:, left : left + 1])
 
-        def group_p(v, part):
-            if part == 0:
-                p_grouped[v] = flow.tile([P, PACK * F], BF16, name="p_grouped", tag="p_grouped", bufs=GROUP_BUFS, align_bytes=64)
-            if part < parts(P_ILV[v]):
-                interleave(P_ILV[v], p_grouped[v], p_planes[v], cols(part, F // 4 // parts(P_ILV[v])))
+        def group_p(e, g, engine):
+            if g == 0:
+                p_grouped[e] = flow.tile([P, HALVES * PACK * F], BF16, name="grouped", tag="grouped", bufs=GROUP_BUFS, align_bytes=64)
+            interleave(engine, p_grouped[e][:, cols(g, PACK * F)], p_planes[e, g][:])
 
         def aggregate(i):
             unit, j = divmod(i, PACK)
             e = unit // HALVES
             agg = bank("mx")
             for g in range(HALVES):
-                mx(agg[:], p_mx[HALVES * e + g], cols(j, P), a_mx[unit], cols(g, HALF), g == 0, g == HALVES - 1)
+                mx(agg[:], p_mx[e], cols(PACK * g + j, P), a_mx[unit], cols(g, HALF), g == 0, g == HALVES - 1)
             if j == 0:
-                h_rows[unit] = flow.tile([P, PACK, HALF], F32, name="h_rows", tag="h_rows", bufs=3, align_bytes=64)
+                h_rows[unit] = flow.tile([P, PACK, HALF], F32, name="h_rows", tag="h_rows", bufs=H_BUFS, align_bytes=64)
             nc.scalar.activation(out=h_rows[unit][:, j, :], in_=agg[:], func=ACT.Relu, bias=b_cols[:, PACK * e + j : PACK * e + j + 1])
 
         def turn_h(i):
@@ -239,10 +232,13 @@ def tile_relationalgraphmixtureofexperts_kernel(tc, x, a_bytes, a_scale, w, c, b
             unit, t = divmod(i, PACK)
             e, h = divmod(unit, HALVES)
             tile = PACK * h + t
-            weight = gate[:, tile, e : e + 1]
+            weight = gate[h][:, t, e : e + 1]
             if e == 0 and not RES_INIT:
                 acc[tile] = keep.tile([P, F], F32, name="acc%d" % tile, align_bytes=64)
-                nc.scalar.activation(out=acc[tile][:], in_=held["h", i][:], func=ACT.Copy, scale=weight)
+                if tile in FIRST_ON_SCALAR:
+                    nc.scalar.activation(out=acc[tile][:], in_=held["h", i][:], func=ACT.Copy, scale=weight)
+                else:
+                    nc.vector.tensor_scalar(out=acc[tile][:], in0=held["h", i][:], scalar1=weight, scalar2=None, op0=ALU.mult)
             else:
                 nc.vector.scalar_tensor_tensor(
                     out=acc[tile][:], in0=held["h", i][:], scalar=weight, in1=acc[tile][:], op0=ALU.mult, op1=ALU.add
@@ -257,111 +253,146 @@ def tile_relationalgraphmixtureofexperts_kernel(tc, x, a_bytes, a_scale, w, c, b
             if RES_INIT:
                 acc[tile] = keep.tile([P, F], F32, name="acc%d" % tile, align_bytes=64)
                 nc.scalar.copy(out=acc[tile][:], in_=res[:])
-            else:
+            elif tile in RES_ON_VECTOR:
                 nc.vector.tensor_tensor(out=acc[tile][:], in0=res[:], in1=acc[tile][:], op=ALU.add)
+            else:
+                direct = flow.tile([P, F], F32, name="direct", tag="direct", bufs=3, align_bytes=64)
+                nc.scalar.copy(out=direct[:], in_=res[:])
+                nc.gpsimd.tensor_tensor(out=acc[tile][:], in0=direct[:], in1=acc[tile][:], op=ALU.add)
 
         c32 = keep.tile([P, HALVES * PACK], F32, name="c32", align_bytes=64)
         b_cols = keep.tile([P, E * PACK], F32, name="b_cols", align_bytes=64)
-        gate = keep.tile([P, HALVES * PACK, E], F32, name="gate", align_bytes=64)
+        gate = [keep.tile([P, PACK, E], F32, name="gate%d" % h, align_bytes=64) for h in range(HALVES)]
+
+        nc.gpsimd.tensor_copy(out=c32[:], in_=c_raw[:].rearrange("p g t -> p (g t)"))
 
         def constants():
-            nc.scalar.copy(out=c32[:], in_=c_raw[:].rearrange("p g t -> p (g t)"))
             nc.scalar.copy(out=b_wide[: E * PACK, :], in_=b_rows[:])
             back = bank("back")
             nc.tensor.transpose(back[:, cols(0, P)], b_wide[:], ident[:])
             nc.scalar.copy(out=b_cols[:], in_=back[:, : E * PACK])
 
         def gate_logits(tile):
-            if tile == 0:
-                logits = bank("back")
-                held["logits"] = logits[:, : HALVES * PACK * E].rearrange("p (n e) -> p n e", e=E)
             h, t = divmod(tile, PACK)
+            if t == 0:
+                logits = flow.tile([P, PACK, E], F32, name="logits", tag="logits", align_bytes=64)
+                held["logits", h] = logits[:]
+            sums = bank("mx")
             planes = x_turned[h][:].rearrange("p (n s) -> p n s", s=PACK)
             for s in range(PACK):
-                nc.tensor.matmul(
-                    held["logits"][:, tile, :], lhsT=planes[:, cols(t, P), s], rhs=wg_sb[:, s, :], start=s == 0, stop=s == PACK - 1
+                nc.tensor.matmul(sums[:, :E], lhsT=planes[:, cols(t, P), s], rhs=wg_sb[:, s, :], start=s == 0, stop=s == PACK - 1)
+            nc.scalar.copy(out=held["logits", h][:, t, :], in_=sums[:, :E])
+
+        shape = [P, PACK, E]
+
+        def softmax_step(h, step):
+            if step == 0:
+                top = flow.tile(shape[:2], F32, name="top", tag="top", align_bytes=64)
+                nc.vector.tensor_reduce(out=top[:], in_=held["logits", h], axis=AX.X, op=ALU.max)
+                held["top"] = top
+            elif step == 1:
+                shifted = flow.tile(shape, F32, name="shifted", tag="shifted", align_bytes=64)
+                nc.vector.tensor_tensor(
+                    out=shifted[:], in0=held["logits", h], in1=held["top"][:].unsqueeze(2).to_broadcast(shape), op=ALU.subtract
+                )
+                expo = flow.tile(shape, F32, name="expo", tag="expo", align_bytes=64)
+                nc.scalar.activation(out=expo[:], in_=shifted[:], func=ACT.Exp)
+                held["expo", h] = expo
+            elif step == 2:
+                total = flow.tile(shape[:2], F32, name="total", tag="total", align_bytes=64)
+                nc.vector.tensor_reduce(out=total[:], in_=held["expo", h][:], axis=AX.X, op=ALU.add)
+                held["total"] = total
+            elif step == 3:
+                inverse = flow.tile(shape[:2], F32, name="inverse", tag="inverse", align_bytes=64)
+                nc.vector.reciprocal(out=inverse[:], in_=held["total"][:])
+                held["inverse"] = inverse
+            else:
+                nc.gpsimd.tensor_tensor(
+                    out=gate[h][:], in0=held["expo", h][:], in1=held["inverse"][:].unsqueeze(2).to_broadcast(shape), op=ALU.mult
                 )
 
-        shape = [P, HALVES * PACK, E]
-        top = keep.tile(shape[:2], F32, name="top", align_bytes=64)
-        shifted = keep.tile(shape, F32, name="shifted", align_bytes=64)
-        expo = keep.tile(shape, F32, name="expo", align_bytes=64)
-        total = keep.tile(shape[:2], F32, name="total", align_bytes=64)
-        inverse = keep.tile(shape[:2], F32, name="inverse", align_bytes=64)
-
-        def softmax_step(step):
-            if step == 0:
-                nc.vector.tensor_reduce(out=top[:], in_=held["logits"], axis=AX.X, op=ALU.max)
-            elif step == 1:
-                nc.vector.tensor_tensor(out=shifted[:], in0=held["logits"], in1=top[:].unsqueeze(2).to_broadcast(shape), op=ALU.subtract)
-                nc.scalar.activation(out=expo[:], in_=shifted[:], func=ACT.Exp)
-            elif step == 2:
-                nc.vector.tensor_reduce(out=total[:], in_=expo[:], axis=AX.X, op=ALU.add)
-            elif step == 3:
-                nc.vector.reciprocal(out=inverse[:], in_=total[:])
-            else:
-                nc.vector.tensor_tensor(out=gate[:], in0=expo[:], in1=inverse[:].unsqueeze(2).to_broadcast(shape), op=ALU.mult)
-
         steps = UNITS * PACK
+        tiles = HALVES * PACK
 
         def due(slot, slots):
             return [i for i, s in enumerate(slots) if s == slot]
 
-        def paced(first, last):
-            return [first + i * (last - first) // (steps - 1) for i in range(steps)]
+        def quantise_p(e):
+            p_mx[e] = quantise(p_grouped[e][:], "p", 2)
 
-        def after(slots, lag):
-            return [s + lag for s in slots[PACK - 1 :: PACK]]
+        def quantise_x(h):
+            x_mx[h] = quantise(x_turned[h][:], "x", 2)
 
-        widen_at = paced(0, WIDEN_LAST)
-        project_at = [PROJ_FIRST + i // PROJ_BURST if i < PROJ_HEAD else PROJ_LAG + i for i in range(steps)]
-        aggregate_at = paced(AGG_FIRST, AGG_LAST)
-        mix_at = paced(AGG_FIRST + MIX_LAG, AGG_LAST + MIX_LAG)
-        w_quant_at = [s - W_QUANT_LEAD for s in project_at[2 * PACK :: 2 * PACK]] + [RES_FIRST - W_QUANT_LEAD]
+        def quantise_a(unit):
+            a_mx[unit] = quantise(a_turned[unit][:], "a", 3)
 
-        p_quant_at = [s + P_GROUP_LAG + P_QUANT_LAG + parts(P_ILV[v]) - 1 for v, s in enumerate(after(project_at, 0))]
-        assert W_GROUP_LEAD >= S_PARTS
-        assert all(RES_FIRST + i < s for i, s in enumerate(mix_at[-HALVES * PACK :]))
-        for slot in range(mix_at[-1] + 1):
-            for i in due(slot, widen_at):
-                widen_a(i)
-            for h in due(slot, range(HALVES)):
-                turn_x(h, 0)
-                turn_x(h, 1)
-            if slot == W0_AT:
-                for part in range(S_PARTS):
-                    group_w(0, part)
-            for i in due(slot + 1, mix_at):
-                turn_h(i)
-            for i in due(slot - 1, widen_at):
-                turn_a(i)
-                copy_a(i)
-            for h in due(slot - 1, range(HALVES)):
-                x_mx[h] = quantise(x_turned[h][:], "x", 2)
-            if slot == W0_AT + 1:
-                w_mx[0] = quantise(w_grouped[0][:], "w", 3)
-            if slot == 1:
-                constants()
-            for i in due(slot, mix_at):
+        def move_a(i):
+            turn_a(i)
+            copy_a(i)
+
+        names = {"I": lambda e: group_w(e, "V"), "W": quantise_w, "a": widen_a, "t": move_a, "X": quantise_x, "p": project,
+                 "x": lambda i: turn_x(i // 2, i % 2), "J": lambda g: group_p(0, g, "V"), "P": quantise_p, "G": lambda e: group_w(e, "G"),
+                 "A": quantise_a, "c": lambda i: constants(), "g": gate_logits, "S": lambda e: group_w(e, "S"),
+                 "m": lambda i: softmax_step(i // 10, i % 10)}
+        for item in PROLOGUE.split():
+            names[item[0]](int(item[1:]))
+
+        project_at = [-1] * (tiles + PACK) + [PROJ_SECOND + i * PROJ_SPAN // PACK for i in range(PACK)]
+        project_at += [i - PROJ_LEAD for i in range(2 * tiles, steps)]
+        mix_at = [i + AGG_LAG + MIX_LAG - sum(1 for m in MIX_CATCH if i >= m) for i in range(steps)]
+        agg_at = [i + AGG_LAG - sum(1 for m in AGG_CATCH if i >= m) for i in range(steps)]
+        a_quant_at = [PACK * u + A_Q - (1 if u >= EARLY_A else 0) for u in range(UNITS)]
+        assert all(mix_at[i] - 1 > agg_at[i // PACK * PACK + PACK - 1] for i in range(steps))
+        for slot in range(FIRST, mix_at[-1] + 1):
+            turns, mixes = due(slot + 1, mix_at), due(slot, mix_at)
+            if slot < steps:
+                widen_a(slot)
+            for i in mixes[:-1]:
                 mix(i)
-            for i in due(slot, aggregate_at):
+            for i in turns[:1]:
+                turn_h(i)
+            for i in due(slot - 1, range(steps)):
+                move_a(i)
+            for i in mixes[-1:]:
+                mix(i)
+            for i in due(slot, agg_at):
                 aggregate(i)
             for i in due(slot, project_at):
                 project(i)
-            for tile in due(slot - RES_FIRST, range(HALVES * PACK)):
+            for tile in due(slot - RES_FIRST, [i + RES_SKIP * (i // 3) for i in range(tiles)]):
                 residual(tile)
-            for tile in due(slot - GATE_LAG, range(HALVES * PACK)):
+            for i in turns[1:]:
+                turn_h(i)
+            for tile in due(slot, GATE_AT):
                 gate_logits(tile)
-            for step in due(slot - GATE_LAG - HALVES * PACK, range(5)):
-                softmax_step(step)
-            for unit in due(slot, after(widen_at, A_QUANT_LAG)):
-                a_mx[unit] = quantise(a_turned[unit][:], "a", 4)
-            for e in due(slot, w_quant_at):
-                w_mx[e + 1] = quantise(w_grouped[e + 1][:], "w", 3)
-            for v in due(slot, p_quant_at):
-                p_mx[v] = quantise(p_grouped[v][:], "p", UNITS)
-            for part in range(S_PARTS):
-                for v in due(slot - part, after(project_at, P_GROUP_LAG)):
-                    group_p(v, part)
-                for e in due(slot - part + W_GROUP_LEAD, w_quant_at):
-                    group_w(e + 1, part)
+            for h in due(slot - A_Q - 1, [PACK * u for u in SM_END]):
+                softmax_step(h, 2)
+                softmax_step(h, 3)
+                softmax_step(h, 4)
+                if h == 0:
+                    group_p(1, 1, P1_ENG[1])
+            if slot == LAST_P:
+                quantise_p(E - 1)
+            for unit in due(slot, a_quant_at):
+                if unit == 0:
+                    continue
+                for h in due(unit, SM_END):
+                    softmax_step(h, 0)
+                quantise_a(unit)
+                for h in due(unit, SM_END):
+                    softmax_step(h, 1)
+                e, h = divmod(unit, HALVES)
+                if unit == RES_UNIT:
+                    quantise_w(E)
+                if h == 0:
+                    if e + 1 < E:
+                        quantise_p(e)
+                    if e + 2 < E:
+                        group_w(e + 2, "G")
+                elif e + 1 < E:
+                    if e + 2 < E:
+                        quantise_w(e + 2)
+                    for g in range(HALVES if e else 1):
+                        group_p(e + 1, g, P1_ENG[g] if e == 0 else "G")
+                if unit == RES_UNIT - 1 and unit > 0:
+                    group_w(E, "G")

@@ -20,37 +20,20 @@ P = 128
 PACK = 4
 HALF = P * PACK
 HALVES = N // HALF
+TILES = HALVES * PACK
 UNITS = E * HALVES
-AGG_LAG = 7
-A_Q = 6
-FIRST = 6
-MIX_LAG = 8
-PROJ_SECOND = 7
-PROJ_SPAN = 4
-PROJ_LEAD = 5
-P1_ENG = "GG"
-RES_FIRST = 11
-RES_UNIT = 1
-RES_INIT = True
-RES_ON_VECTOR = ()
-RES_SKIP = 1
-FIRST_ON_SCALAR = ()
-GATE_AT = (-1, -1, 6, 6, 9, 10, 11, 12)
-SM_END = (1, 2)
+ITEMS = UNITS * PACK
+DIRECT = E
+
+QUANT_LAG = PACK + 2
+AGGREGATE_LAG = QUANT_LAG + 1
+MIX_LAG = 2 * AGGREGATE_LAG
+FIRST_STEP = AGGREGATE_LAG
+SECOND_QUANT = PACK + QUANT_LAG
+A_BUFS = 4
 WIDE_BUFS = 6
-H_BUFS = 4
-GROUP_BUFS = 1
-PROLOGUE = 'I0 x0 x1 a0 a1 x2 x3 c0 X0 a2 X1 W0 G1 t0 t1 p0 p1 p2 p3 p4 p5 p6 p7 a3 a4 t2 t3 a5 W1 J0 g0 g1 p8 p9 p10 p11 J1 A0 t4 P0 G2 G4'
-BANKS = {"turn": 2, "mx": 2, "back": 2}
-HEAD_LOADS = 'w0 x0 x1 a0'
-REST_LOADS = 'w1 a1 w2 w4 a2 a3 w3'
-SHARED = 4
-RING_W = True
-AGG_CATCH = (21,)
-EARLY_A = 6
-LAST_P = 29
-MIX_CATCH = (18, 22)
-S_PSUM = True
+TO_SCALAR_BANKS = 4
+TO_VECTOR_BANKS = 2
 
 
 def tile_relationalgraphmixtureofexperts_kernel(tc, x, a_bytes, a_scale, w, c, b, wg, w0, out):
@@ -58,22 +41,32 @@ def tile_relationalgraphmixtureofexperts_kernel(tc, x, a_bytes, a_scale, w, c, b
     with ExitStack() as ctx:
         keep = ctx.enter_context(tc.tile_pool(name="keep", bufs=1))
         flow = ctx.enter_context(tc.tile_pool(name="flow", bufs=2))
-        psum = ctx.enter_context(tc.psum_pool(name="psum", bufs=2))
+        psum = ctx.enter_context(tc.psum_pool(name="psum", bufs=1))
         ctx.enter_context(tc.manual_schedule())
 
-        def bank(tag):
-            if SHARED and tag != "back":
-                return psum.tile([P, HALF], F32, name="any", tag="any", bufs=SHARED)
-            return psum.tile([P, HALF], F32, name=tag, tag=tag, bufs=BANKS[tag])
+        def cols(i, width):
+            return slice(i * width, (i + 1) * width)
+
+        def kept(name, shape, dtype):
+            return keep.tile(shape, dtype, name=name, align_bytes=64)
+
+        def ring(tag, shape, dtype, bufs):
+            return flow.tile(shape, dtype, name=tag, tag=tag, bufs=bufs, align_bytes=64)
+
+        def scalar_bank():
+            return psum.tile([P, HALF], F32, name="to_scalar", tag="to_scalar", bufs=TO_SCALAR_BANKS)
+
+        def vector_bank():
+            return psum.tile([P, HALF], F32, name="to_vector", tag="to_vector", bufs=TO_VECTOR_BANKS)
 
         def quantise(grouped, tag, bufs):
             width = grouped.shape[1] // PACK
-            codes = flow.tile([P, width], U32, name=tag + "_codes", tag=tag + "_codes", bufs=bufs, align_bytes=64)
-            scales = flow.tile([P, width], U8, name=tag + "_scales", tag=tag + "_scales", bufs=bufs, align_bytes=64)
-            nc.vector.quantize_mx(out=codes[:].bitcast(FP8X4), scales=scales[:], in_=grouped)
-            return codes, scales
+            words = ring(tag + "_words", [P, width], U32, bufs)
+            scales = ring(tag + "_scales", [P, width], U8, bufs)
+            nc.vector.quantize_mx(out=words[:].bitcast(FP8X4), scales=scales[:], in_=grouped)
+            return words, scales
 
-        def mx(dst, still, still_cols, moving, moving_cols, start, stop):
+        def mx_pass(dst, still, still_cols, moving, moving_cols, start, stop):
             nc.tensor.matmul_mx(
                 out=dst,
                 lhsT=still[0][:, still_cols].bitcast(FP8X4),
@@ -84,315 +77,312 @@ def tile_relationalgraphmixtureofexperts_kernel(tc, x, a_bytes, a_scale, w, c, b
                 stop=stop,
             )
 
-        def cols(i, width):
-            return slice(i * width, (i + 1) * width)
+        def interleave_on_vector(grouped, planes):
+            nc.vector.tensor_copy(
+                out=grouped.rearrange("p (n i t) -> p n t i", i=4, t=PACK), in_=planes.rearrange("p t (n i) -> p n t i", i=4)
+            )
 
-        def interleave(engine, grouped, planes):
-            if engine == "G":
-                dst = grouped.rearrange("p (n t) -> p n t", t=PACK)
-                src = planes.rearrange("p t n -> p n t")
-                nc.gpsimd.tensor_scalar(out=dst, in0=src, scalar1=1.0, scalar2=0.0, op0=ALU.mult, op1=ALU.add)
-            else:
-                dst = grouped.rearrange("p (c i t) -> p c t i", i=4, t=PACK)
-                src = planes.rearrange("p t (c i) -> p c t i", i=4)
-                if engine == "S":
-                    nc.scalar.copy(out=dst, in_=src)
-                else:
-                    nc.vector.tensor_copy(out=dst, in_=src)
+        def interleave_on_gpsimd(grouped, planes):
+            nc.gpsimd.tensor_scalar(
+                out=grouped.rearrange("p (n t) -> p n t", t=PACK),
+                in0=planes.rearrange("p t n -> p n t"),
+                scalar1=1.0,
+                scalar2=0.0,
+                op0=ALU.mult,
+                op1=ALU.add,
+            )
 
-        a_raw, w_raw, x_raw = {}, {}, {}
-
-        def load_a(unit):
-            e, h = divmod(unit, HALVES)
-            a_raw[unit] = flow.tile([P, PACK * N], U8, name="a_raw", tag="a_raw", bufs=4, align_bytes=64)
-            nc.sync.dma_start(out=a_raw[unit][:], in_=a_bytes[e, cols(h, HALF), :].rearrange("(p t) m -> p (t m)", t=PACK))
-
-        def load_w(e):
-            src = w0 if e == E else w[e]
-            w_raw[e] = keep.tile([P, PACK, F], BF16, name="w_raw%d" % e, align_bytes=64)
-            nc.sync.dma_start(out=w_raw[e][:], in_=src.rearrange("(p t) f -> p t f", t=PACK))
-
-        def load_x(h):
-            x_raw[h] = keep.tile([P, PACK, D], BF16, name="x_raw%d" % h, align_bytes=64)
-            nc.sync.dma_start(out=x_raw[h][:], in_=x[cols(h, HALF), :].rearrange("(p t) d -> p t d", t=PACK))
-
-        ident = keep.tile([P, P], F32, name="ident", align_bytes=64)
+        ident = kept("ident", [P, P], F32)
         make_identity(nc, ident[:])
-        b_wide = keep.tile([P, P], F32, name="b_wide", align_bytes=64)
+        wg_wide = kept("wg_wide", [P, PACK, P], BF16)
+        nc.gpsimd.memset(wg_wide[:], 0.0)
+        b_wide = kept("b_wide", [P, P], F32)
         nc.gpsimd.memset(b_wide[:], 0.0)
 
-        s_cols = keep.tile([P, HALVES, PACK], F32, name="s_cols", align_bytes=64)
-        nc.sync.dma_start(out=s_cols[:], in_=a_scale.rearrange("i j (g p t) -> p (i j g) t", p=P, t=PACK))
-        for item in HEAD_LOADS.split():
-            {"a": load_a, "x": load_x, "w": load_w}[item[0]](int(item[1]))
-        wg_sb = keep.tile([P, PACK, E], BF16, name="wg_sb", align_bytes=64)
-        nc.sync.dma_start(out=wg_sb[:], in_=wg.rearrange("(p t) e -> p t e", t=PACK))
-        c_raw = keep.tile([P, HALVES, PACK], BF16, name="c_raw", align_bytes=64)
-        nc.sync.dma_start(out=c_raw[:], in_=c.rearrange("(g p t) -> p g t", p=P, t=PACK))
-        b_rows = keep.tile([E * PACK, P], BF16, name="b_rows", align_bytes=64)
-        nc.sync.dma_start(out=b_rows[:], in_=b.rearrange("e (j p) -> (e j) p", p=P))
-        for item in REST_LOADS.split():
-            {"a": load_a, "x": load_x, "w": load_w}[item[0]](int(item[1]))
+        a_raw, w_planes, x_rows = {}, {}, {}
 
-        s_half = []
+        def load_a(unit, parts=1):
+            e, h = divmod(unit, HALVES)
+            a_raw[unit] = ring("a_raw", [P, PACK * N], U8, A_BUFS)
+            rows = a_bytes[e, cols(h, HALF), :].rearrange("(p t) m -> p (t m)", t=PACK)
+            width = PACK * N // parts
+            return [(a_raw[unit][:, cols(i, width)], rows[:, cols(i, width)]) for i in range(parts)]
+
+        def load_w(e):
+            w_planes[e] = kept("w_planes%d" % e, [P, PACK, F], BF16)
+            return [(w_planes[e][:], (w0 if e == DIRECT else w[e]).rearrange("(p t) f -> p t f", t=PACK))]
+
+        def load_x(pair):
+            x_rows[pair] = kept("x_rows%d" % pair, [P, 2, D], BF16)
+            rows = x[cols(pair // 2, HALF), :].rearrange("(p t) d -> p t d", t=PACK)
+            return [(x_rows[pair][:], rows[:, cols(pair % 2, 2), :])]
+
+        def issue(loads):
+            for dst, src in loads:
+                nc.sync.dma_start(out=dst, in_=src)
+
+        s_cols = kept("s_cols", [P, HALVES, PACK], F32)
+        c_raw = kept("c_raw", [P, HALVES, PACK], BF16)
+        b_rows = kept("b_rows", [E * PACK, P], BF16)
+        a_first = load_a(0, parts=2)
+        issue([(s_cols[:], a_scale.rearrange("i j (g p t) -> p (i j g) t", p=P, t=PACK))])
+        issue(load_w(0) + load_x(0) + load_x(1) + a_first[:1] + load_x(2) + load_x(3) + a_first[1:])
+        issue([(wg_wide[:, :, :E], wg.rearrange("(p t) e -> p t e", t=PACK))])
+        issue([(c_raw[:], c.rearrange("(g p t) -> p g t", p=P, t=PACK))])
+        issue([(b_rows[:], b.rearrange("e (j p) -> (e j) p", p=P))])
+        issue(load_a(1) + load_w(1) + load_w(2) + load_w(DIRECT) + load_a(2) + load_a(3) + load_w(3))
+
+        s_spread = []
         for g in range(HALVES):
-            spread = psum.tile([P, HALF], F32, name="s_spread%d" % g, bufs=1)
+            spread = psum.tile([P, HALF], F32, name="s_spread%d" % g)
             for t in range(PACK):
                 nc.tensor.transpose(spread[:, t::PACK], s_cols[:, g, t : t + 1].to_broadcast([P, P]), ident[:])
-            s_half.append(spread[:])
+            s_spread.append(spread)
 
-        a_wide, a_turned, a_mx = {}, {}, {}
-        x_turned, x_mx, w_grouped, w_mx = {}, {}, {}, {}
-        p_planes, p_grouped, p_mx, h_rows, acc = {}, {}, {}, {}, {}
-        held = {}
+        c32 = kept("c32", [P, TILES], F32)
+        nc.gpsimd.tensor_copy(out=c32[:], in_=c_raw[:].rearrange("p g t -> p (g t)"))
 
-        def widen_a(i):
-            unit, t = divmod(i, PACK)
-            a_wide[i] = flow.tile([P, N], BF16, name="a_wide", tag="a_wide", bufs=WIDE_BUFS, align_bytes=64)
-            codes = a_raw[unit][:, cols(t, N)].bitcast(FP8)
+        a_wide, a_grouped, a_mx = {}, {}, {}
+        x_grouped, x_mx, w_grouped, w_mx = {}, {}, {}, {}
+        p_planes, p_grouped, p_mx = {}, {}, {}
+        h_cols, h_turned, acc, logit_rows = {}, {}, {}, {}
+
+        def turn_words(dst, words):
+            for u in range(2):
+                nc.tensor.transpose(dst[:, cols(u, P)], words[:, u::2], ident[:])
+
+        def turn_x(pair):
+            h, first = divmod(2 * pair, PACK)
+            bank = scalar_bank()
+            for i in range(2):
+                turn_words(bank[:, cols(i, 2 * P)], x_rows[pair][:, i, :].bitcast(F32))
+            if first == 0:
+                x_grouped[h] = kept("x_grouped%d" % h, [P, PACK * HALF], BF16)
+            dst = x_grouped[h][:].bitcast(F32).rearrange("p (t r u) -> p t r u", t=PACK, u=2)
+            nc.scalar.copy(out=dst[:, first : first + 2], in_=bank[:].rearrange("p (i u r) -> p i r u", i=2, u=2))
+
+        def quantise_x(h):
+            x_mx[h] = quantise(x_grouped[h][:], "x", HALVES)
+
+        def widen_a(item):
+            unit, t = divmod(item, PACK)
+            a_wide[item] = ring("a_wide", [P, N], BF16, WIDE_BUFS)
+            values = a_raw[unit][:, cols(t, N)].bitcast(FP8)
             for g in range(HALVES):
-                nc.vector.tensor_tensor(out=a_wide[i][:, cols(g, HALF)], in0=codes[:, cols(g, HALF)], in1=s_half[g], op=ALU.mult)
-            if t == PACK - 1 and unit + 4 < UNITS:
-                load_a(unit + 4)
+                nc.vector.tensor_tensor(
+                    out=a_wide[item][:, cols(g, HALF)], in0=values[:, cols(g, HALF)], in1=s_spread[g][:], op=ALU.mult
+                )
+            if t == PACK - 1 and unit + A_BUFS < UNITS:
+                issue(load_a(unit + A_BUFS))
 
-        def turn_a(i):
-            words = a_wide[i][:].bitcast(F32)
-            turned = bank("turn")
+        def turn_a(item):
+            unit, t = divmod(item, PACK)
+            bank = scalar_bank()
             for g in range(HALVES):
-                for u in range(2):
-                    nc.tensor.transpose(turned[:, cols(2 * g + u, P)], words[:, 2 * P * g + u : 2 * P * (g + 1) : 2], ident[:])
-            held["a", i] = turned
-
-        def copy_a(i):
-            unit, t = divmod(i, PACK)
+                turn_words(bank[:, cols(g, 2 * P)], a_wide[item][:, cols(g, HALF)].bitcast(F32))
             if t == 0:
-                a_turned[unit] = flow.tile([P, PACK * N], BF16, name="a_turned", tag="a_turned", bufs=2, align_bytes=64)
-            dst = a_turned[unit][:].bitcast(F32).rearrange("p (g t r u) -> p g t r u", g=HALVES, t=PACK, u=2)
-            nc.scalar.copy(out=dst[:, :, t], in_=held["a", i][:].rearrange("p (g u r) -> p g r u", g=HALVES, u=2))
+                a_grouped[unit] = ring("a_grouped", [P, PACK * N], BF16, 2)
+            dst = a_grouped[unit][:].bitcast(F32).rearrange("p (g t r u) -> p g t r u", g=HALVES, t=PACK, u=2)
+            nc.scalar.copy(out=dst[:, :, t], in_=bank[:].rearrange("p (g u r) -> p g r u", g=HALVES, u=2))
 
-        def turn_x(h, pair):
-            words = x_raw[h][:].bitcast(F32)
-            turned = bank("turn")
-            for s in range(2):
-                for u in range(2):
-                    nc.tensor.transpose(turned[:, cols(2 * s + u, P)], words[:, 2 * pair + s, u::2], ident[:])
-            if pair == 0:
-                x_turned[h] = keep.tile([P, PACK * HALF], BF16, name="x_turned%d" % h, align_bytes=64)
-            dst = x_turned[h][:].bitcast(F32).rearrange("p (t r u) -> p t r u", t=PACK, u=2)
-            nc.scalar.copy(out=dst[:, 2 * pair : 2 * pair + 2], in_=turned[:].rearrange("p (s u r) -> p s r u", s=2, u=2))
+        def quantise_a(unit):
+            a_mx[unit] = quantise(a_grouped[unit][:], "a", 3)
 
-        def group_w(e, engine):
-            if e == E:
-                w_grouped[e] = keep.tile([P, PACK * F], BF16, name="w4_grouped", align_bytes=64)
-            elif e < 2 and not RING_W:
-                w_grouped[e] = keep.tile([P, PACK * F], BF16, name="w%d_grouped" % e, align_bytes=64)
-            else:
-                w_grouped[e] = flow.tile([P, HALVES * PACK * F], BF16, name="grouped", tag="grouped", bufs=GROUP_BUFS, align_bytes=64)
-            interleave(engine, w_grouped[e][:, : PACK * F], w_raw[e][:])
+        def shared_buffer():
+            return ring("grouped", [P, HALVES * PACK * F], BF16, 1)
+
+        def group_w(e, interleave):
+            w_grouped[e] = kept("w0_grouped", [P, PACK * F], BF16) if e == DIRECT else shared_buffer()
+            interleave(w_grouped[e][:, : PACK * F], w_planes[e][:])
 
         def quantise_w(e):
             w_mx[e] = quantise(w_grouped[e][:, : PACK * F], "w", 3)
 
-        def project(i):
-            e, left = divmod(i, HALVES * PACK)
-            g, t = divmod(left, PACK)
-            proj = bank("mx")
-            mx(proj[:], x_mx[g], cols(t, P), w_mx[e], cols(0, F), True, True)
+        def project(item):
+            e, tile = divmod(item, TILES)
+            g, t = divmod(tile, PACK)
+            bank = scalar_bank()
+            mx_pass(bank[:], x_mx[g], cols(t, P), w_mx[e], cols(0, F), True, True)
             if t == 0:
-                p_planes[e, g] = flow.tile([P, PACK, F], BF16, name="p_planes", tag="p_planes", bufs=3, align_bytes=64)
-            nc.scalar.activation(out=p_planes[e, g][:, t, :], in_=proj[:], func=ACT.Copy, scale=c32[:, left : left + 1])
+                p_planes[e, g] = ring("p_planes", [P, PACK, F], BF16, 3)
+            nc.scalar.activation(out=p_planes[e, g][:, t, :], in_=bank[:], func=ACT.Copy, scale=c32[:, tile : tile + 1])
 
-        def group_p(e, g, engine):
+        def group_p(e, g, interleave):
             if g == 0:
-                p_grouped[e] = flow.tile([P, HALVES * PACK * F], BF16, name="grouped", tag="grouped", bufs=GROUP_BUFS, align_bytes=64)
-            interleave(engine, p_grouped[e][:, cols(g, PACK * F)], p_planes[e, g][:])
-
-        def aggregate(i):
-            unit, j = divmod(i, PACK)
-            e = unit // HALVES
-            agg = bank("mx")
-            for g in range(HALVES):
-                mx(agg[:], p_mx[e], cols(PACK * g + j, P), a_mx[unit], cols(g, HALF), g == 0, g == HALVES - 1)
-            if j == 0:
-                h_rows[unit] = flow.tile([P, PACK, HALF], F32, name="h_rows", tag="h_rows", bufs=H_BUFS, align_bytes=64)
-            nc.scalar.activation(out=h_rows[unit][:, j, :], in_=agg[:], func=ACT.Relu, bias=b_cols[:, PACK * e + j : PACK * e + j + 1])
-
-        def turn_h(i):
-            unit, t = divmod(i, PACK)
-            back = bank("back")
-            for j in range(PACK):
-                nc.tensor.transpose(back[:, cols(j, P)], h_rows[unit][:, j, cols(t, P)], ident[:])
-            held["h", i] = back
-
-        def store(tile):
-            h, t = divmod(tile, PACK)
-            nc.sync.dma_start(out=out[cols(h, HALF), :].rearrange("(p t) f -> p t f", t=PACK)[:, t, :], in_=acc[tile][:])
-
-        def mix(i):
-            unit, t = divmod(i, PACK)
-            e, h = divmod(unit, HALVES)
-            tile = PACK * h + t
-            weight = gate[h][:, t, e : e + 1]
-            if e == 0 and not RES_INIT:
-                acc[tile] = keep.tile([P, F], F32, name="acc%d" % tile, align_bytes=64)
-                if tile in FIRST_ON_SCALAR:
-                    nc.scalar.activation(out=acc[tile][:], in_=held["h", i][:], func=ACT.Copy, scale=weight)
-                else:
-                    nc.vector.tensor_scalar(out=acc[tile][:], in0=held["h", i][:], scalar1=weight, scalar2=None, op0=ALU.mult)
-            else:
-                nc.vector.scalar_tensor_tensor(
-                    out=acc[tile][:], in0=held["h", i][:], scalar=weight, in1=acc[tile][:], op0=ALU.mult, op1=ALU.add
-                )
-            if e == E - 1:
-                store(tile)
-
-        def residual(tile):
-            h, t = divmod(tile, PACK)
-            res = bank("mx")
-            mx(res[:], x_mx[h], cols(t, P), w_mx[E], cols(0, F), True, True)
-            if RES_INIT:
-                acc[tile] = keep.tile([P, F], F32, name="acc%d" % tile, align_bytes=64)
-                nc.scalar.copy(out=acc[tile][:], in_=res[:])
-            elif tile in RES_ON_VECTOR:
-                nc.vector.tensor_tensor(out=acc[tile][:], in0=res[:], in1=acc[tile][:], op=ALU.add)
-            else:
-                direct = flow.tile([P, F], F32, name="direct", tag="direct", bufs=3, align_bytes=64)
-                nc.scalar.copy(out=direct[:], in_=res[:])
-                nc.gpsimd.tensor_tensor(out=acc[tile][:], in0=direct[:], in1=acc[tile][:], op=ALU.add)
-
-        c32 = keep.tile([P, HALVES * PACK], F32, name="c32", align_bytes=64)
-        b_cols = keep.tile([P, E * PACK], F32, name="b_cols", align_bytes=64)
-        gate = [keep.tile([P, PACK, E], F32, name="gate%d" % h, align_bytes=64) for h in range(HALVES)]
-
-        nc.gpsimd.tensor_copy(out=c32[:], in_=c_raw[:].rearrange("p g t -> p (g t)"))
-
-        def constants():
-            nc.scalar.copy(out=b_wide[: E * PACK, :], in_=b_rows[:])
-            back = bank("back")
-            nc.tensor.transpose(back[:, cols(0, P)], b_wide[:], ident[:])
-            nc.scalar.copy(out=b_cols[:], in_=back[:, : E * PACK])
-
-        def gate_logits(tile):
-            h, t = divmod(tile, PACK)
-            if t == 0:
-                logits = flow.tile([P, PACK, E], F32, name="logits", tag="logits", align_bytes=64)
-                held["logits", h] = logits[:]
-            sums = bank("mx")
-            planes = x_turned[h][:].rearrange("p (n s) -> p n s", s=PACK)
-            for s in range(PACK):
-                nc.tensor.matmul(sums[:, :E], lhsT=planes[:, cols(t, P), s], rhs=wg_sb[:, s, :], start=s == 0, stop=s == PACK - 1)
-            nc.scalar.copy(out=held["logits", h][:, t, :], in_=sums[:, :E])
-
-        shape = [P, PACK, E]
-
-        def softmax_step(h, step):
-            if step == 0:
-                top = flow.tile(shape[:2], F32, name="top", tag="top", align_bytes=64)
-                nc.vector.tensor_reduce(out=top[:], in_=held["logits", h], axis=AX.X, op=ALU.max)
-                held["top"] = top
-            elif step == 1:
-                shifted = flow.tile(shape, F32, name="shifted", tag="shifted", align_bytes=64)
-                nc.vector.tensor_tensor(
-                    out=shifted[:], in0=held["logits", h], in1=held["top"][:].unsqueeze(2).to_broadcast(shape), op=ALU.subtract
-                )
-                expo = flow.tile(shape, F32, name="expo", tag="expo", align_bytes=64)
-                nc.scalar.activation(out=expo[:], in_=shifted[:], func=ACT.Exp)
-                held["expo", h] = expo
-            elif step == 2:
-                total = flow.tile(shape[:2], F32, name="total", tag="total", align_bytes=64)
-                nc.vector.tensor_reduce(out=total[:], in_=held["expo", h][:], axis=AX.X, op=ALU.add)
-                held["total"] = total
-            elif step == 3:
-                inverse = flow.tile(shape[:2], F32, name="inverse", tag="inverse", align_bytes=64)
-                nc.vector.reciprocal(out=inverse[:], in_=held["total"][:])
-                held["inverse"] = inverse
-            else:
-                nc.gpsimd.tensor_tensor(
-                    out=gate[h][:], in0=held["expo", h][:], in1=held["inverse"][:].unsqueeze(2).to_broadcast(shape), op=ALU.mult
-                )
-
-        steps = UNITS * PACK
-        tiles = HALVES * PACK
-
-        def due(slot, slots):
-            return [i for i, s in enumerate(slots) if s == slot]
+                p_grouped[e] = shared_buffer()
+            interleave(p_grouped[e][:, cols(g, PACK * F)], p_planes[e, g][:])
 
         def quantise_p(e):
             p_mx[e] = quantise(p_grouped[e][:], "p", 2)
 
-        def quantise_x(h):
-            x_mx[h] = quantise(x_turned[h][:], "x", 2)
+        def aggregate(item):
+            unit, j = divmod(item, PACK)
+            e = unit // HALVES
+            bank = scalar_bank()
+            for g in range(HALVES):
+                mx_pass(bank[:], p_mx[e], cols(PACK * g + j, P), a_mx[unit], cols(g, HALF), g == 0, g == HALVES - 1)
+            if j == 0:
+                h_cols[unit] = ring("h_cols", [P, PACK, HALF], F32, 3)
+            bias = b_cols[:, PACK * e + j : PACK * e + j + 1]
+            nc.scalar.activation(out=h_cols[unit][:, j, :], in_=bank[:], func=ACT.Relu, bias=bias)
 
-        def quantise_a(unit):
-            a_mx[unit] = quantise(a_turned[unit][:], "a", 3)
+        def turn_h(item, take_bank=vector_bank):
+            unit, t = divmod(item, PACK)
+            h_turned[item] = take_bank()
+            for j in range(PACK):
+                nc.tensor.transpose(h_turned[item][:, cols(j, P)], h_cols[unit][:, j, cols(t, P)], ident[:])
 
-        def move_a(i):
-            turn_a(i)
-            copy_a(i)
+        def direct(tile):
+            h, t = divmod(tile, PACK)
+            bank = scalar_bank()
+            mx_pass(bank[:], x_mx[h], cols(t, P), w_mx[DIRECT], cols(0, F), True, True)
+            acc[tile] = kept("acc%d" % tile, [P, F], F32)
+            nc.scalar.copy(out=acc[tile][:], in_=bank[:])
 
-        names = {"I": lambda e: group_w(e, "V"), "W": quantise_w, "a": widen_a, "t": move_a, "X": quantise_x, "p": project,
-                 "x": lambda i: turn_x(i // 2, i % 2), "J": lambda g: group_p(0, g, "V"), "P": quantise_p, "G": lambda e: group_w(e, "G"),
-                 "A": quantise_a, "c": lambda i: constants(), "g": gate_logits, "S": lambda e: group_w(e, "S"),
-                 "m": lambda i: softmax_step(i // 10, i % 10)}
-        for item in PROLOGUE.split():
-            names[item[0]](int(item[1:]))
+        def mix(item):
+            e, tile = divmod(item, TILES)
+            nc.vector.scalar_tensor_tensor(
+                out=acc[tile][:],
+                in0=h_turned[item][:],
+                scalar=gate[:, tile, e : e + 1],
+                in1=acc[tile][:],
+                op0=ALU.mult,
+                op1=ALU.add,
+            )
+            if e == E - 1:
+                h, t = divmod(tile, PACK)
+                nc.sync.dma_start(out=out[cols(h, HALF), :].rearrange("(p t) f -> p t f", t=PACK)[:, t, :], in_=acc[tile][:])
 
-        project_at = [-1] * (tiles + PACK) + [PROJ_SECOND + i * PROJ_SPAN // PACK for i in range(PACK)]
-        project_at += [i - PROJ_LEAD for i in range(2 * tiles, steps)]
-        mix_at = [i + AGG_LAG + MIX_LAG - sum(1 for m in MIX_CATCH if i >= m) for i in range(steps)]
-        agg_at = [i + AGG_LAG - sum(1 for m in AGG_CATCH if i >= m) for i in range(steps)]
-        a_quant_at = [PACK * u + A_Q - (1 if u >= EARLY_A else 0) for u in range(UNITS)]
-        assert all(mix_at[i] - 1 > agg_at[i // PACK * PACK + PACK - 1] for i in range(steps))
-        for slot in range(FIRST, mix_at[-1] + 1):
-            turns, mixes = due(slot + 1, mix_at), due(slot, mix_at)
-            if slot < steps:
-                widen_a(slot)
-            for i in mixes[:-1]:
-                mix(i)
-            for i in turns[:1]:
-                turn_h(i)
-            for i in due(slot - 1, range(steps)):
-                move_a(i)
-            for i in mixes[-1:]:
-                mix(i)
-            for i in due(slot, agg_at):
-                aggregate(i)
-            for i in due(slot, project_at):
-                project(i)
-            for tile in due(slot - RES_FIRST, [i + RES_SKIP * (i // 3) for i in range(tiles)]):
-                residual(tile)
-            for i in turns[1:]:
-                turn_h(i)
-            for tile in due(slot, GATE_AT):
-                gate_logits(tile)
-            for h in due(slot - A_Q - 1, [PACK * u for u in SM_END]):
-                softmax_step(h, 2)
-                softmax_step(h, 3)
-                softmax_step(h, 4)
-                if h == 0:
-                    group_p(1, 1, P1_ENG[1])
-            if slot == LAST_P:
-                quantise_p(E - 1)
-            for unit in due(slot, a_quant_at):
-                if unit == 0:
-                    continue
-                for h in due(unit, SM_END):
-                    softmax_step(h, 0)
+        per_node = [P, TILES, E]
+        b_cols = kept("b_cols", [P, E * PACK], F32)
+        logits = kept("logits", per_node, F32)
+        top = kept("top", per_node[:2], F32)
+        shifted = kept("shifted", per_node, F32)
+        expo = kept("expo", per_node, F32)
+        total = kept("total", per_node[:2], F32)
+        inverse = kept("inverse", per_node[:2], F32)
+        gate = kept("gate", per_node, F32)
+
+        def turn_bias():
+            bank = vector_bank()
+            nc.tensor.transpose(bank[:, cols(0, P)], b_wide[:], ident[:])
+            nc.scalar.copy(out=b_cols[:], in_=bank[:, : E * PACK])
+
+        def gate_sums(h):
+            bank = vector_bank()
+            planes = x_grouped[h][:].rearrange("p (n t) -> p t n", t=PACK)
+            for t in range(PACK):
+                nc.tensor.matmul(bank[:], lhsT=wg_wide[:, t, :], rhs=planes[:, t, :], start=t == 0, stop=t == PACK - 1)
+            logit_rows[h] = ring("logit_rows", [P, HALF], F32, HALVES)
+            nc.scalar.copy(out=logit_rows[h][:], in_=bank[:])
+
+        def turn_logits(h):
+            bank = vector_bank()
+            for t in range(PACK):
+                nc.tensor.transpose(bank[:, cols(t, P)], logit_rows[h][:, cols(t, P)], ident[:])
+            nc.scalar.copy(out=logits[:, cols(h, PACK), :], in_=bank[:].rearrange("p (t m) -> p t m", t=PACK)[:, :, :E])
+
+        def over_experts(column):
+            return column[:].unsqueeze(2).to_broadcast(per_node)
+
+        group_w(0, interleave_on_vector)
+        turn_x(0)
+        turn_x(1)
+        widen_a(0)
+        widen_a(1)
+        turn_x(2)
+        turn_x(3)
+        for h in range(HALVES):
+            gate_sums(h)
+        nc.scalar.copy(out=b_wide[: E * PACK, :], in_=b_rows[:])
+        turn_a(0)
+        turn_a(1)
+        for h in range(HALVES):
+            widen_a(2 + h)
+            quantise_x(h)
+        quantise_w(0)
+        group_w(1, interleave_on_gpsimd)
+        for item in range(TILES):
+            project(item)
+        turn_a(2)
+        turn_a(3)
+        turn_bias()
+        for h in range(HALVES):
+            turn_logits(h)
+        for item in range(PACK, FIRST_STEP):
+            widen_a(item)
+        quantise_w(1)
+        group_p(0, 0, interleave_on_vector)
+        for item in range(TILES, TILES + PACK):
+            project(item)
+        group_p(0, 1, interleave_on_vector)
+        quantise_a(0)
+        for item in range(PACK, FIRST_STEP - 1):
+            turn_a(item)
+        nc.vector.tensor_reduce(out=top[:], in_=logits[:], axis=AX.X, op=ALU.max)
+        quantise_p(0)
+        nc.vector.tensor_tensor(out=shifted[:], in0=logits[:], in1=over_experts(top), op=ALU.subtract)
+        nc.scalar.activation(out=expo[:], in_=shifted[:], func=ACT.Exp)
+        group_w(2, interleave_on_gpsimd)
+        group_w(DIRECT, interleave_on_gpsimd)
+
+        def quantise_round(unit):
+            e, h = divmod(unit, HALVES)
+            if unit == 1:
+                nc.vector.tensor_reduce(out=total[:], in_=expo[:], axis=AX.X, op=ALU.add)
                 quantise_a(unit)
-                for h in due(unit, SM_END):
-                    softmax_step(h, 1)
-                e, h = divmod(unit, HALVES)
-                if unit == RES_UNIT:
-                    quantise_w(E)
-                if h == 0:
-                    if e + 1 < E:
-                        quantise_p(e)
-                    if e + 2 < E:
-                        group_w(e + 2, "G")
-                elif e + 1 < E:
-                    if e + 2 < E:
-                        quantise_w(e + 2)
-                    for g in range(HALVES if e else 1):
-                        group_p(e + 1, g, P1_ENG[g] if e == 0 else "G")
-                if unit == RES_UNIT - 1 and unit > 0:
-                    group_w(E, "G")
+                nc.vector.reciprocal(out=inverse[:], in_=total[:])
+                quantise_w(DIRECT)
+                nc.vector.tensor_tensor(out=gate[:], in0=expo[:], in1=over_experts(inverse), op=ALU.mult)
+            else:
+                quantise_a(unit)
+            if h == 0 and e + 1 < E:
+                quantise_p(e)
+                if e + 2 < E:
+                    group_w(e + 2, interleave_on_gpsimd)
+            elif h == 1:
+                if e + 2 < E:
+                    quantise_w(e + 2)
+                for g in range(HALVES):
+                    group_p(e + 1, g, interleave_on_gpsimd)
+
+        project_lead = TILES + PACK - FIRST_STEP
+        last_p_step = PACK * (UNITS - HALVES) + QUANT_LAG - 1
+        for step in range(FIRST_STEP, ITEMS):
+            widen_a(step)
+            if step + 1 >= MIX_LAG:
+                turn_h(step + 1 - MIX_LAG)
+            turn_a(step - 1)
+            if step >= MIX_LAG:
+                mix(step - MIX_LAG)
+            aggregate(step - AGGREGATE_LAG)
+            if step + project_lead < ITEMS:
+                project(step + project_lead)
+            if 0 <= step - SECOND_QUANT - 1 < TILES:
+                direct(step - SECOND_QUANT - 1)
+            if step == last_p_step:
+                quantise_p(E - 1)
+            if (step - QUANT_LAG) % PACK == 0:
+                quantise_round((step - QUANT_LAG) // PACK)
+
+        last_unit = ITEMS - PACK
+        mixed = ITEMS - MIX_LAG
+        turn_a(ITEMS - 1)
+        turn_h(mixed + 1)
+        mix(mixed)
+        for item in range(ITEMS - AGGREGATE_LAG, last_unit):
+            aggregate(item)
+        mix(mixed + 1)
+        quantise_a(UNITS - 1)
+        pairs = [(i, i + 1) for i in range(mixed + 2, ITEMS, 2)]
+        for item in pairs[0]:
+            turn_h(item)
+        for n, pair in enumerate(pairs):
+            if n + 1 < len(pairs):
+                for item in pairs[n + 1]:
+                    turn_h(item, vector_bank if n % 2 else scalar_bank)
+            for item in pair:
+                mix(item)
+            if 2 * n < PACK:
+                aggregate(last_unit + 2 * n)
+                aggregate(last_unit + 2 * n + 1)

@@ -315,6 +315,7 @@ def tile_relationalgraphmixtureofexperts_kernel(tc, x, a_bytes, a_scale, w, c, b
         group_p(0, 0, interleave_on_vector)
         for item in range(TILES, TILES + PACK):
             project(item)
+        group_w(DIRECT, interleave_on_vector)
         group_p(0, 1, interleave_on_vector)
         quantise_a(0)
         for item in range(PACK, FIRST_STEP - 1):
@@ -324,7 +325,6 @@ def tile_relationalgraphmixtureofexperts_kernel(tc, x, a_bytes, a_scale, w, c, b
         nc.vector.tensor_tensor(out=shifted[:], in0=logits[:], in1=over_experts(top), op=ALU.subtract)
         nc.scalar.activation(out=expo[:], in_=shifted[:], func=ACT.Exp)
         group_w(2, interleave_on_gpsimd)
-        group_w(DIRECT, interleave_on_gpsimd)
 
         def quantise_round(unit):
             e, h = divmod(unit, HALVES)

from contextlib import ExitStack

import concourse.mybir as mybir
from concourse.masks import make_identity

N, D, F, E = 1024, 512, 512, 4
FLOPS = 2 * N * D * F * (E + 1) + 2 * E * N * N * F + 2 * N * D * E

F32 = mybir.dt.float32
BF16 = mybir.dt.bfloat16
U32 = mybir.dt.uint32
U8 = mybir.dt.uint8
FP8 = mybir.dt.float8_e4m3fn
FP8X4 = mybir.dt.float8_e4m3fn_x4
ALU = mybir.AluOpType
ACT = mybir.ActivationFunctionType
AX = mybir.AxisListType

P = 128
PACK = 4
HALF = P * PACK
HALVES = N // HALF
TILES = HALVES * PACK
UNITS = E * HALVES
ITEMS = UNITS * PACK
DIRECT = E

QUANT_LAG = PACK + 2
AGGREGATE_LAG = QUANT_LAG + 1
MIX_LAG = 2 * AGGREGATE_LAG
FIRST_STEP = AGGREGATE_LAG
SECOND_QUANT = PACK + QUANT_LAG
A_BUFS = 4
WIDE_BUFS = 6
TO_SCALAR_BANKS = 4
TO_VECTOR_BANKS = 2


def tile_relationalgraphmixtureofexperts_kernel(tc, x, a_bytes, a_scale, w, c, b, wg, w0, out):
    nc = tc.nc
    with ExitStack() as ctx:
        keep = ctx.enter_context(tc.tile_pool(name="keep", bufs=1))
        flow = ctx.enter_context(tc.tile_pool(name="flow", bufs=2))
        psum = ctx.enter_context(tc.psum_pool(name="psum", bufs=1))
        ctx.enter_context(tc.manual_schedule())

        def cols(i, width):
            return slice(i * width, (i + 1) * width)

        def kept(name, shape, dtype):
            return keep.tile(shape, dtype, name=name, align_bytes=64)

        def ring(tag, shape, dtype, bufs):
            return flow.tile(shape, dtype, name=tag, tag=tag, bufs=bufs, align_bytes=64)

        def scalar_bank():
            return psum.tile([P, HALF], F32, name="to_scalar", tag="to_scalar", bufs=TO_SCALAR_BANKS)

        def vector_bank():
            return psum.tile([P, HALF], F32, name="to_vector", tag="to_vector", bufs=TO_VECTOR_BANKS)

        def quantise(grouped, tag, bufs):
            width = grouped.shape[1] // PACK
            words = ring(tag + "_words", [P, width], U32, bufs)
            scales = ring(tag + "_scales", [P, width], U8, bufs)
            nc.vector.quantize_mx(out=words[:].bitcast(FP8X4), scales=scales[:], in_=grouped)
            return words, scales

        def mx_pass(dst, still, still_cols, moving, moving_cols, start, stop):
            nc.tensor.matmul_mx(
                out=dst,
                lhsT=still[0][:, still_cols].bitcast(FP8X4),
                lhsT_scale=still[1][:, still_cols],
                rhs=moving[0][:, moving_cols].bitcast(FP8X4),
                rhs_scale=moving[1][:, moving_cols],
                start=start,
                stop=stop,
            )

        def interleave_on_vector(grouped, planes):
            nc.vector.tensor_copy(
                out=grouped.rearrange("p (n i t) -> p n t i", i=4, t=PACK), in_=planes.rearrange("p t (n i) -> p n t i", i=4)
            )

        def interleave_on_gpsimd(grouped, planes):
            nc.gpsimd.tensor_scalar(
                out=grouped.rearrange("p (n t) -> p n t", t=PACK),
                in0=planes.rearrange("p t n -> p n t"),
                scalar1=1.0,
                scalar2=0.0,
                op0=ALU.mult,
                op1=ALU.add,
            )

        ident = kept("ident", [P, P], F32)
        make_identity(nc, ident[:])
        wg_wide = kept("wg_wide", [P, PACK, P], BF16)
        nc.gpsimd.memset(wg_wide[:], 0.0)
        b_wide = kept("b_wide", [P, P], F32)
        nc.gpsimd.memset(b_wide[:], 0.0)

        a_raw, w_planes, x_rows = {}, {}, {}

        def load_a(unit, parts=1):
            e, h = divmod(unit, HALVES)
            a_raw[unit] = ring("a_raw", [P, PACK * N], U8, A_BUFS)
            rows = a_bytes[e, cols(h, HALF), :].rearrange("(p t) m -> p (t m)", t=PACK)
            width = PACK * N // parts
            return [(a_raw[unit][:, cols(i, width)], rows[:, cols(i, width)]) for i in range(parts)]

        def load_w(e):
            w_planes[e] = kept("w_planes%d" % e, [P, PACK, F], BF16)
            return [(w_planes[e][:], (w0 if e == DIRECT else w[e]).rearrange("(p t) f -> p t f", t=PACK))]

        def load_x(pair):
            x_rows[pair] = kept("x_rows%d" % pair, [P, 2, D], BF16)
            rows = x[cols(pair // 2, HALF), :].rearrange("(p t) d -> p t d", t=PACK)
            return [(x_rows[pair][:], rows[:, cols(pair % 2, 2), :])]

        def issue(loads):
            for dst, src in loads:
                nc.sync.dma_start(out=dst, in_=src)

        s_cols = kept("s_cols", [P, HALVES, PACK], F32)
        c_raw = kept("c_raw", [P, HALVES, PACK], BF16)
        b_rows = kept("b_rows", [E * PACK, P], BF16)
        a_first = load_a(0, parts=2)
        issue([(s_cols[:], a_scale.rearrange("i j (g p t) -> p (i j g) t", p=P, t=PACK))])
        issue(load_w(0) + load_x(0) + load_x(1) + a_first[:1] + load_x(2) + load_x(3) + a_first[1:])
        issue([(wg_wide[:, :, :E], wg.rearrange("(p t) e -> p t e", t=PACK))])
        issue([(c_raw[:], c.rearrange("(g p t) -> p g t", p=P, t=PACK))])
        issue([(b_rows[:], b.rearrange("e (j p) -> (e j) p", p=P))])
        issue(load_a(1) + load_w(1) + load_w(2) + load_w(DIRECT) + load_a(2) + load_a(3) + load_w(3))

        s_spread = []
        for g in range(HALVES):
            spread = psum.tile([P, HALF], F32, name="s_spread%d" % g)
            for t in range(PACK):
                nc.tensor.transpose(spread[:, t::PACK], s_cols[:, g, t : t + 1].to_broadcast([P, P]), ident[:])
            s_spread.append(spread)

        c32 = kept("c32", [P, TILES], F32)
        nc.gpsimd.tensor_copy(out=c32[:], in_=c_raw[:].rearrange("p g t -> p (g t)"))

        a_wide, a_grouped, a_mx = {}, {}, {}
        x_grouped, x_mx, w_grouped, w_mx = {}, {}, {}, {}
        p_planes, p_grouped, p_mx = {}, {}, {}
        h_cols, h_turned, acc, logit_rows = {}, {}, {}, {}

        def turn_words(dst, words):
            for u in range(2):
                nc.tensor.transpose(dst[:, cols(u, P)], words[:, u::2], ident[:])

        def turn_x(pair):
            h, first = divmod(2 * pair, PACK)
            bank = scalar_bank()
            for i in range(2):
                turn_words(bank[:, cols(i, 2 * P)], x_rows[pair][:, i, :].bitcast(F32))
            if first == 0:
                x_grouped[h] = kept("x_grouped%d" % h, [P, PACK * HALF], BF16)
            dst = x_grouped[h][:].bitcast(F32).rearrange("p (t r u) -> p t r u", t=PACK, u=2)
            nc.scalar.copy(out=dst[:, first : first + 2], in_=bank[:].rearrange("p (i u r) -> p i r u", i=2, u=2))

        def quantise_x(h):
            x_mx[h] = quantise(x_grouped[h][:], "x", HALVES)

        def widen_a(item):
            unit, t = divmod(item, PACK)
            a_wide[item] = ring("a_wide", [P, N], BF16, WIDE_BUFS)
            values = a_raw[unit][:, cols(t, N)].bitcast(FP8)
            for g in range(HALVES):
                nc.vector.tensor_tensor(
                    out=a_wide[item][:, cols(g, HALF)], in0=values[:, cols(g, HALF)], in1=s_spread[g][:], op=ALU.mult
                )
            if t == PACK - 1 and unit + A_BUFS < UNITS:
                issue(load_a(unit + A_BUFS))

        def turn_a(item):
            unit, t = divmod(item, PACK)
            bank = scalar_bank()
            for g in range(HALVES):
                turn_words(bank[:, cols(g, 2 * P)], a_wide[item][:, cols(g, HALF)].bitcast(F32))
            if t == 0:
                a_grouped[unit] = ring("a_grouped", [P, PACK * N], BF16, 2)
            dst = a_grouped[unit][:].bitcast(F32).rearrange("p (g t r u) -> p g t r u", g=HALVES, t=PACK, u=2)
            nc.scalar.copy(out=dst[:, :, t], in_=bank[:].rearrange("p (g u r) -> p g r u", g=HALVES, u=2))

        def quantise_a(unit):
            a_mx[unit] = quantise(a_grouped[unit][:], "a", 3)

        def shared_buffer():
            return ring("grouped", [P, HALVES * PACK * F], BF16, 1)

        def group_w(e, interleave):
            w_grouped[e] = kept("w0_grouped", [P, PACK * F], BF16) if e == DIRECT else shared_buffer()
            interleave(w_grouped[e][:, : PACK * F], w_planes[e][:])

        def quantise_w(e):
            w_mx[e] = quantise(w_grouped[e][:, : PACK * F], "w", 3)

        def project(item):
            e, tile = divmod(item, TILES)
            g, t = divmod(tile, PACK)
            bank = scalar_bank()
            mx_pass(bank[:], x_mx[g], cols(t, P), w_mx[e], cols(0, F), True, True)
            if t == 0:
                p_planes[e, g] = ring("p_planes", [P, PACK, F], BF16, 3)
            nc.scalar.activation(out=p_planes[e, g][:, t, :], in_=bank[:], func=ACT.Copy, scale=c32[:, tile : tile + 1])

        def group_p(e, g, interleave):
            if g == 0:
                p_grouped[e] = shared_buffer()
            interleave(p_grouped[e][:, cols(g, PACK * F)], p_planes[e, g][:])

        def quantise_p(e):
            p_mx[e] = quantise(p_grouped[e][:], "p", 2)

        def aggregate(item):
            unit, j = divmod(item, PACK)
            e = unit // HALVES
            bank = scalar_bank()
            for g in range(HALVES):
                mx_pass(bank[:], p_mx[e], cols(PACK * g + j, P), a_mx[unit], cols(g, HALF), g == 0, g == HALVES - 1)
            if j == 0:
                h_cols[unit] = ring("h_cols", [P, PACK, HALF], F32, 3)
            bias = b_cols[:, PACK * e + j : PACK * e + j + 1]
            nc.scalar.activation(out=h_cols[unit][:, j, :], in_=bank[:], func=ACT.Relu, bias=bias)

        def turn_h(item, take_bank=vector_bank):
            unit, t = divmod(item, PACK)
            h_turned[item] = take_bank()
            for j in range(PACK):
                nc.tensor.transpose(h_turned[item][:, cols(j, P)], h_cols[unit][:, j, cols(t, P)], ident[:])

        def direct(tile):
            h, t = divmod(tile, PACK)
            bank = scalar_bank()
            mx_pass(bank[:], x_mx[h], cols(t, P), w_mx[DIRECT], cols(0, F), True, True)
            acc[tile] = kept("acc%d" % tile, [P, F], F32)
            nc.scalar.copy(out=acc[tile][:], in_=bank[:])

        def mix(item):
            e, tile = divmod(item, TILES)
            nc.vector.scalar_tensor_tensor(
                out=acc[tile][:],
                in0=h_turned[item][:],
                scalar=gate[:, tile, e : e + 1],
                in1=acc[tile][:],
                op0=ALU.mult,
                op1=ALU.add,
            )
            if e == E - 1:
                h, t = divmod(tile, PACK)
                nc.sync.dma_start(out=out[cols(h, HALF), :].rearrange("(p t) f -> p t f", t=PACK)[:, t, :], in_=acc[tile][:])

        per_node = [P, TILES, E]
        b_cols = kept("b_cols", [P, E * PACK], F32)
        logits = kept("logits", per_node, F32)
        top = kept("top", per_node[:2], F32)
        shifted = kept("shifted", per_node, F32)
        expo = kept("expo", per_node, F32)
        total = kept("total", per_node[:2], F32)
        inverse = kept("inverse", per_node[:2], F32)
        gate = kept("gate", per_node, F32)

        def turn_bias():
            bank = vector_bank()
            nc.tensor.transpose(bank[:, cols(0, P)], b_wide[:], ident[:])
            nc.scalar.copy(out=b_cols[:], in_=bank[:, : E * PACK])

        def gate_sums(h):
            bank = vector_bank()
            planes = x_grouped[h][:].rearrange("p (n t) -> p t n", t=PACK)
            for t in range(PACK):
                nc.tensor.matmul(bank[:], lhsT=wg_wide[:, t, :], rhs=planes[:, t, :], start=t == 0, stop=t == PACK - 1)
            logit_rows[h] = ring("logit_rows", [P, HALF], F32, HALVES)
            nc.scalar.copy(out=logit_rows[h][:], in_=bank[:])

        def turn_logits(h):
            bank = vector_bank()
            for t in range(PACK):
                nc.tensor.transpose(bank[:, cols(t, P)], logit_rows[h][:, cols(t, P)], ident[:])
            nc.scalar.copy(out=logits[:, cols(h, PACK), :], in_=bank[:].rearrange("p (t m) -> p t m", t=PACK)[:, :, :E])

        def over_experts(column):
            return column[:].unsqueeze(2).to_broadcast(per_node)

        group_w(0, interleave_on_vector)
        turn_x(0)
        turn_x(1)
        widen_a(0)
        widen_a(1)
        turn_x(2)
        turn_x(3)
        for h in range(HALVES):
            gate_sums(h)
        nc.scalar.copy(out=b_wide[: E * PACK, :], in_=b_rows[:])
        turn_a(0)
        turn_a(1)
        for h in range(HALVES):
            widen_a(2 + h)
            quantise_x(h)
        quantise_w(0)
        group_w(1, interleave_on_gpsimd)
        for item in range(TILES):
            project(item)
        turn_a(2)
        turn_a(3)
        turn_bias()
        for h in range(HALVES):
            turn_logits(h)
        for item in range(PACK, FIRST_STEP):
            widen_a(item)
        quantise_w(1)
        group_p(0, 0, interleave_on_vector)
        for item in range(TILES, TILES + PACK):
            project(item)
        group_w(DIRECT, interleave_on_vector)
        group_p(0, 1, interleave_on_vector)
        quantise_a(0)
        for item in range(PACK, FIRST_STEP - 1):
            turn_a(item)
        nc.vector.tensor_reduce(out=top[:], in_=logits[:], axis=AX.X, op=ALU.max)
        quantise_p(0)
        nc.vector.tensor_tensor(out=shifted[:], in0=logits[:], in1=over_experts(top), op=ALU.subtract)
        nc.scalar.activation(out=expo[:], in_=shifted[:], func=ACT.Exp)
        group_w(2, interleave_on_gpsimd)

        def quantise_round(unit):
            e, h = divmod(unit, HALVES)
            if unit == 1:
                nc.vector.tensor_reduce(out=total[:], in_=expo[:], axis=AX.X, op=ALU.add)
                quantise_a(unit)
                nc.vector.reciprocal(out=inverse[:], in_=total[:])
                quantise_w(DIRECT)
                nc.vector.tensor_tensor(out=gate[:], in0=expo[:], in1=over_experts(inverse), op=ALU.mult)
            else:
                quantise_a(unit)
            if h == 0 and e + 1 < E:
                quantise_p(e)
                if e + 2 < E:
                    group_w(e + 2, interleave_on_gpsimd)
            elif h == 1:
                if e + 2 < E:
                    quantise_w(e + 2)
                for g in range(HALVES):
                    group_p(e + 1, g, interleave_on_gpsimd)

        project_lead = TILES + PACK - FIRST_STEP
        last_p_step = PACK * (UNITS - HALVES) + QUANT_LAG - 1
        for step in range(FIRST_STEP, ITEMS):
            widen_a(step)
            if step + 1 >= MIX_LAG:
                turn_h(step + 1 - MIX_LAG)
            turn_a(step - 1)
            if step >= MIX_LAG:
                mix(step - MIX_LAG)
            aggregate(step - AGGREGATE_LAG)
            if step + project_lead < ITEMS:
                project(step + project_lead)
            if 0 <= step - SECOND_QUANT - 1 < TILES:
                direct(step - SECOND_QUANT - 1)
            if step == last_p_step:
                quantise_p(E - 1)
            if (step - QUANT_LAG) % PACK == 0:
                quantise_round((step - QUANT_LAG) // PACK)

        last_unit = ITEMS - PACK
        mixed = ITEMS - MIX_LAG
        turn_a(ITEMS - 1)
        turn_h(mixed + 1)
        mix(mixed)
        for item in range(ITEMS - AGGREGATE_LAG, last_unit):
            aggregate(item)
        mix(mixed + 1)
        quantise_a(UNITS - 1)
        pairs = [(i, i + 1) for i in range(mixed + 2, ITEMS, 2)]
        for item in pairs[0]:
            turn_h(item)
        for n, pair in enumerate(pairs):
            if n + 1 < len(pairs):
                for item in pairs[n + 1]:
                    turn_h(item, vector_bank if n % 2 else scalar_bank)
            for item in pair:
                mix(item)
            if 2 * n < PACK:
                aggregate(last_unit + 2 * n)
                aggregate(last_unit + 2 * n + 1)
